import numpy as np
import ml_dtypes


def mxq(x, axis, fmt="e4m3"):
    dtype, down = {"e4m3": (ml_dtypes.float8_e4m3fn, 7), "e5m2": (ml_dtypes.float8_e5m2, 14)}[fmt]
    v = np.moveaxis(np.asarray(x, np.float32).astype(ml_dtypes.bfloat16).astype(np.float64), axis, -1)
    blocks = v.reshape(v.shape[:-1] + (-1, 32))
    amax = np.abs(blocks).max(-1, keepdims=True)
    byte = np.maximum(np.where(amax > 0, np.frexp(amax)[1] - 1 + 127, 0) - down, 1)
    scale = np.exp2(byte - 127.0)
    codes = (blocks / scale).astype(np.float32).astype(dtype).astype(np.float64)
    return np.moveaxis((codes * scale).reshape(v.shape), -1, axis)


WIDE = False


def mx_kscale(k):
    if not WIDE:
        return np.ones(k)
    levels = np.array([10, -10, 5, -5, 0])
    if k % 512:
        return np.exp2(np.random.permutation(np.resize(levels, k // 32))).repeat(32)
    a = np.empty((k // 512, 16))
    for p in range(k // 512):
        a[p, :8] = np.random.permutation(np.resize(levels, 8))
        for g in range(8):
            far = levels[np.abs(levels - a[p, g]) >= 10]
            a[p, g + 8] = far[np.random.randint(len(far))]
    return np.exp2(a.ravel()).repeat(32)


def f64(x):
    return np.asarray(x).astype(np.float64)


def striped(idx):
    return np.tile(np.asarray(idx).reshape(-1, 16).T, (8, 1)).astype(np.uint16)


def unstriped(offs):
    return offs[:16].T.reshape(-1).astype(np.int64)


E2M1 = np.array([0.0, 0.5, 1.0, 1.5, 2.0, 3.0, 4.0, 6.0, -0.0, -0.5, -1.0, -1.5, -2.0, -3.0, -4.0, -6.0])


def pack_weight(w, fmt):
    k, n = w.shape
    w = f64(np.asarray(w, np.float32).astype(ml_dtypes.bfloat16)).reshape(k // 32, 32, n)
    amax = np.abs(w).max(1)
    if fmt == "e4m3":
        byte = np.frexp(amax)[1] - 1 + 127 - 7
    else:
        mant, ex = np.frexp(amax / 6.0)
        byte = np.where(mant > 0.5, ex, ex - 1) + 127
    byte = np.clip(np.where(amax > 0, byte, 1), 1, 254)
    scaled = (w * np.exp2(127.0 - byte)[:, None, :]).reshape(k, n).astype(np.float32)
    by_word = np.ascontiguousarray(scaled.reshape(k // 512, 128, 4, n).transpose(0, 1, 3, 2))
    if fmt == "e4m3":
        words = by_word.astype(ml_dtypes.float8_e4m3fn).view(np.uint8)
    else:
        c = by_word.astype(ml_dtypes.float4_e2m1fn).view(np.uint8) & 0xF
        words = (c[..., 0::2] | (c[..., 1::2] << 4)).reshape(k // 512, 128, 2 * n)
    return np.ascontiguousarray(words), np.ascontiguousarray(byte.astype(np.uint8).reshape(k // 512, 16, n))


def unpack_weight(words, scales, fmt):
    g, _, n = scales.shape
    words = np.ascontiguousarray(words).reshape(g, 128, n, -1)
    if fmt == "e4m3":
        vals = words.view(ml_dtypes.float8_e4m3fn).astype(np.float64)
    else:
        nib = np.empty((g, 128, n, 4), np.uint8)
        nib[..., 0::2] = words & 0xF
        nib[..., 1::2] = words >> 4
        vals = E2M1[nib]
    vals = vals * np.repeat(np.exp2(scales.astype(np.float64) - 127.0), 8, axis=1)[..., None]
    return vals.transpose(0, 1, 3, 2).reshape(g * 512, n)


D, I, Q, E, U = 512, 512, 128, 512, 512


def setup_inputs():
    n = np.random.standard_normal
    idx = np.random.randint(0, U, I)
    idx2 = np.random.randint(0, U, I)
    idx3 = np.random.randint(0, U, I)
    fd = mx_kscale(D)
    fi = mx_kscale(I)
    bap = pack_weight(n((D, U)) / fd[:, None], "e4m3")
    bbp = pack_weight(n((D, U)) * 0.6 / fd[:, None], "e4m3")
    bcp = pack_weight(n((D, U)) * 0.4 / fd[:, None], "e4m3")
    return {
        "query": (n((D, Q)) * 0.25 / np.sqrt(D) * fd[:, None]).astype(np.float32),
        "ba_words": bap[0],
        "ba_scales": bap[1],
        "bb_words": bbp[0],
        "bb_scales": bbp[1],
        "bc_words": bcp[0],
        "bc_scales": bcp[1],
        "size": (np.random.uniform(0.5, 2.0, (1, I)) * fi).astype(np.float32),
        "ca": (n((E, U))).astype(np.float32),
        "cb": (n((E, U)) * 0.6).astype(np.float32),
        "cc": (n((E, U)) * 0.4).astype(np.float32),
        "vsc": (np.random.uniform(0.5, 2.0, (I, 1)) / fi[:, None]).astype(np.float32),
        "offs": striped(idx),
        "offs2": striped(idx2),
        "offs3": striped(idx3),
    }


def reference(query, ba_words, ba_scales, bb_words, bb_scales, bc_words, bc_scales, size, ca, cb, cc, vsc, offs, offs2, offs3):
    idx = unstriped(offs)
    idx2 = unstriped(offs2)
    idx3 = unstriped(offs3)
    bau = unpack_weight(ba_words, ba_scales, "e4m3")
    bbu = unpack_weight(bb_words, bb_scales, "e4m3")
    bcu = unpack_weight(bc_words, bc_scales, "e4m3")
    queryq = mxq(f64(query), 0, "e4m3")
    baidxg = bau[:, idx]
    bbidx2g = bbu[:, idx2]
    bcidx3g = bcu[:, idx3]
    a = queryq.T @ baidxg + queryq.T @ bbidx2g + queryq.T @ bcidx3g
    p = np.exp(a - np.max(a, axis=1, keepdims=True))
    w = p * f64(size) / np.sum(p, axis=1, keepdims=True)
    wt = w.T
    va = f64(ca)[:, idx].T
    vb = f64(cb)[:, idx2].T
    vc = f64(cc)[:, idx3].T
    vv = (va + vb + vc) * f64(vsc)
    wtq = mxq(wt, 0, "e4m3")
    vvq = mxq(vv, 0, "e4m3")
    o = wtq.T @ vvq
    return o

@@ -1,0 +1,171 @@
+from contextlib import ExitStack
+
+import concourse.mybir as mybir
+from concourse.masks import make_identity
+
+D, I, Q, E, U = 512, 512, 128, 512, 512
+FLOPS = 2 * Q * I * D * 3 + 2 * Q * I * E
+
+F32 = mybir.dt.float32
+BF16 = mybir.dt.bfloat16
+I32 = mybir.dt.int32
+U32 = mybir.dt.uint32
+U16 = mybir.dt.uint16
+U8 = mybir.dt.uint8
+FP8X4 = mybir.dt.float8_e4m3fn_x4
+ACT = mybir.ActivationFunctionType
+ALU = mybir.AluOpType
+
+P = 128
+PACK = 4
+RUN = 8
+BLOCKS = 16
+SPARE = 192
+WINDOW = U + SPARE
+E_TILES = E // P
+
+
+def tile_attend_additivekeys_kernel(tc, query, ba_words, ba_scales, bb_words, bb_scales, bc_words, bc_scales,
+                                     size, ca, cb, cc, vsc, offs, offs2, offs3, out):
+    nc = tc.nc
+    lists_in = (offs, offs2, offs3)
+    words_in = (ba_words, bb_words, bc_words)
+    scales_in = (ba_scales, bb_scales, bc_scales)
+    values_in = (ca, cb, cc)
+    books = range(3)
+
+    with ExitStack() as ctx:
+        keep = ctx.enter_context(tc.tile_pool(name="keep", bufs=1))
+        ring = ctx.enter_context(tc.tile_pool(name="ring", bufs=2))
+        psum = ctx.enter_context(tc.psum_pool(name="psum", bufs=1))
+        psum2 = ctx.enter_context(tc.psum_pool(name="psum2", bufs=2))
+
+        lists = [keep.tile([P, I // 16], U16, name="list%d" % k) for k in books]
+        key_words = [keep.tile([P, WINDOW], I32, name="key_words%d" % k) for k in books]
+        key_scales = [keep.tile([P, WINDOW], U8, name="key_scales%d" % k) for k in books]
+        tables = [keep.tile([P, E_TILES * U + SPARE], F32, name="table%d" % k) for k in books]
+
+        for k in books:
+            nc.vector.memset(key_scales[k][:].bitcast(I32), 0)
+        for k in books:
+            nc.vector.memset(tables[k][:, E_TILES * U:], 0.0)
+        for k in books:
+            nc.vector.memset(key_words[k][:, U:], 0)
+
+        def load_values(k, g):
+            nc.sync.dma_start(out=tables[k][:, g * U:(g + 1) * U], in_=values_in[k][g * P:(g + 1) * P, :])
+
+        last = E_TILES - 1
+        for k in books:
+            nc.sync.dma_start(lists[k][:], lists_in[k])
+            load_values(k, last)
+        for k in books:
+            nc.sync.dma_start(out=key_words[k][:, :U],
+                              in_=words_in[k][0].rearrange("p n t -> p (n t)").bitcast(I32))
+        q_raw = keep.tile([P, PACK, Q], F32)
+        nc.sync.dma_start(out=q_raw[:], in_=query.rearrange("(p j) w -> p j w", j=PACK))
+        for k in books:
+            for quad in range(4):
+                nc.sync.dma_start(out=key_scales[k][32 * quad:32 * quad + 4, :U].bitcast(I32),
+                                  in_=scales_in[k][0, 4 * quad:4 * quad + 4, :].bitcast(I32))
+
+        factor_rows = keep.tile([P, P], F32)
+        nc.gpsimd.memset(factor_rows[:], 0.0)
+        nc.sync.dma_start(out=factor_rows[0:PACK, :].rearrange("t (b j) -> t b j", j=RUN),
+                          in_=vsc.rearrange("(b t j) o -> t b (j o)", t=PACK, j=RUN))
+        nc.sync.dma_start(out=factor_rows[PACK:2 * PACK, :].rearrange("t (b j) -> t b j", j=RUN),
+                          in_=size.rearrange("o (b t j) -> (o t) b j", t=PACK, j=RUN))
+        for g in reversed(range(last)):
+            for k in books:
+                load_values(k, g)
+
+        ident = keep.tile([P, P], F32)
+        make_identity(nc, ident[:])
+
+        factor_bank = psum.tile([P, P], F32)
+        nc.tensor.transpose(factor_bank[:], factor_rows[:], ident[:])
+        factors = keep.tile([P, 2 * PACK], F32)
+        nc.scalar.copy(out=factors[:], in_=factor_bank[:, :2 * PACK])
+
+        q_bf = keep.tile([P, Q, PACK], BF16, align_bytes=64)
+        nc.scalar.copy(out=q_bf[:], in_=q_raw[:].rearrange("p j w -> p w j"))
+        q_codes = keep.tile([P, Q], U32, align_bytes=64)
+        q_scale = keep.tile([P, Q], U8, align_bytes=64)
+
+        def gather_values(g):
+            bank = psum2.tile([P, PACK * P], F32, name="value_bank")
+            for k in books:
+                picked = ring.tile([P, I], F32, name="picked%d" % k)
+                window = tables[k][:, g * U:g * U + WINDOW].bitcast(U32)
+                nc.vector.tensor_copy(
+                    out=picked[:].bitcast(U32).rearrange("p (t b j) -> p b t j", t=PACK, j=RUN),
+                    in_=window.indirect(lists[k][:]))
+                for t in range(PACK):
+                    nc.tensor.matmul(bank[:, t * P:(t + 1) * P], lhsT=picked[:, t * P:(t + 1) * P], rhs=ident[:],
+                                     is_transpose=True, start=(k == 0 and t == 0), stop=(k == 2 and t == PACK - 1))
+            return bank
+
+        def scale_on_scalar(bank, first, name):
+            woven = keep.tile([P, P, PACK], BF16, name=name, align_bytes=64)
+            for t in range(PACK):
+                nc.scalar.activation(out=woven[:, :, t], in_=bank[:, t * P:(t + 1) * P], func=ACT.Copy,
+                                     scale=factors[:, first + t:first + t + 1])
+            return woven
+
+        def quantise(woven, name):
+            codes = keep.tile([P, P], U32, name=name + "_codes", align_bytes=64)
+            plane = keep.tile([P, P], U8, name=name + "_plane", align_bytes=64)
+            nc.vector.quantize_mx(out=codes[:].bitcast(FP8X4), scales=plane[:],
+                                  in_=woven[:].rearrange("p x t -> p (x t)"))
+            return codes, plane
+
+        banks = {last: gather_values(last)}
+        woven_v = {last: scale_on_scalar(banks[last], 0, "vv%d" % last)}
+
+        picked_words = [keep.tile([P, I], U32, name="picked_words%d" % k, align_bytes=64) for k in books]
+        picked_scales = [keep.tile([P, I], U8, name="picked_scales%d" % k, align_bytes=64) for k in books]
+        for k in books:
+            nc.vector.tensor_copy(out=picked_words[k][:], in_=key_words[k][:].bitcast(U32).indirect(lists[k][:]))
+        nc.vector.quantize_mx(out=q_codes[:].bitcast(FP8X4), scales=q_scale[:],
+                              in_=q_bf[:].rearrange("p w j -> p (w j)"))
+        scores = psum.tile([P, I], F32)
+        for k in books:
+            nc.vector.tensor_copy(out=picked_scales[k][:], in_=key_scales[k][:].indirect(lists[k][:]))
+            nc.tensor.matmul_mx(out=scores[:], lhsT=q_codes[:].bitcast(FP8X4), lhsT_scale=q_scale[:],
+                                rhs=picked_words[k][:].bitcast(FP8X4), rhs_scale=picked_scales[k][:],
+                                start=(k == 0), stop=(k == 2))
+
+        neg_max = keep.tile([P, 1], F32)
+        nc.vector.tensor_reduce(out=neg_max[:], in_=scores[:], axis=mybir.AxisListType.X, op=ALU.max, negate=True)
+        prob = keep.tile([P, I], F32)
+        row_sum = keep.tile([P, 1], F32)
+        nc.scalar.activation(out=prob[:], in_=scores[:], func=ACT.Exp, bias=neg_max[:], accum_out=row_sum[:])
+        inv_sum = keep.tile([P, 1], F32)
+        nc.vector.reciprocal(out=inv_sum[:], in_=row_sum[:])
+        prob_dealt = keep.tile([P, I], F32)
+        nc.scalar.activation(out=prob_dealt[:].rearrange("p (t b j) -> p t b j", t=PACK, j=RUN),
+                             in_=prob[:].rearrange("p (b t j) -> p t b j", t=PACK, j=RUN),
+                             func=ACT.Copy, scale=inv_sum[:])
+        weight_bank = psum.tile([P, PACK * P], F32)
+        for t in range(PACK):
+            nc.tensor.transpose(weight_bank[:, t * P:(t + 1) * P], prob_dealt[:, t * P:(t + 1) * P], ident[:])
+        w_codes, w_plane = quantise(scale_on_scalar(weight_bank, PACK, "wt"), "wt")
+
+        def finish(g, woven):
+            codes, plane = quantise(woven, "vv%d" % g)
+            result_bank = psum2.tile([P, P], F32, name="result_bank")
+            nc.tensor.matmul_mx(out=result_bank[:], lhsT=w_codes[:].bitcast(FP8X4), lhsT_scale=w_plane[:],
+                                rhs=codes[:].bitcast(FP8X4), rhs_scale=plane[:], start=True, stop=True)
+            result = ring.tile([P, P], F32, name="result")
+            nc.scalar.copy(out=result[:], in_=result_bank[:])
+            nc.sync.dma_start(out=out[:, g * P:(g + 1) * P], in_=result[:])
+
+        finish(last, woven_v[last])
+        for g in reversed(range(1, last)):
+            finish(g, scale_on_scalar(gather_values(g), 0, "vv%d" % g))
+        bank = gather_values(0)
+        woven = keep.tile([P, P, PACK], BF16, name="vv0", align_bytes=64)
+        nc.vector.tensor_tensor(out=woven[:], in0=bank[:].rearrange("p (t e) -> p e t", t=PACK),
+                                in1=factors[:, 0:PACK].rearrange("p (o t) -> p o t", o=1).to_broadcast([P, P, PACK]),
+                                op=ALU.mult)
+        finish(0, woven)

@@ -43,31 +43,40 @@ def tile_attend_additivekeys_kernel(tc, query, ba_words, ba_scales, bb_words, bb
         lists = [keep.tile([P, I // 16], U16, name="list%d" % k) for k in books]
         key_words = [keep.tile([P, WINDOW], I32, name="key_words%d" % k) for k in books]
         key_scales = [keep.tile([P, WINDOW], U8, name="key_scales%d" % k) for k in books]
-        tables = [keep.tile([P, E_TILES * U + SPARE], F32, name="table%d" % k) for k in books]
+        tables = [keep.tile([P, E_TILES * U + SPARE], F32, name="table%d" % k, tag="table%d" % k, align_bytes=64) for k in books]
 
         for k in books:
-            nc.vector.memset(key_scales[k][:].bitcast(I32), 0)
-        for k in books:
-            nc.vector.memset(tables[k][:, E_TILES * U:], 0.0)
+            nc.gpsimd.memset(key_scales[k][:].bitcast(I32), 0)
         for k in books:
             nc.vector.memset(key_words[k][:, U:], 0)
+        for k in books:
+            nc.vector.memset(tables[k][:, E_TILES * U:], 0.0)
 
         def load_values(k, g):
             nc.sync.dma_start(out=tables[k][:, g * U:(g + 1) * U], in_=values_in[k][g * P:(g + 1) * P, :])
 
-        last = E_TILES - 1
-        for k in books:
-            nc.sync.dma_start(lists[k][:], lists_in[k])
-            load_values(k, last)
-        for k in books:
+        def load_scales(k, queue):
+            for quad in range(4):
+                queue.dma_start(out=key_scales[k][32 * quad:32 * quad + 4, :U].bitcast(I32),
+                                  in_=scales_in[k][0, 4 * quad:4 * quad + 4, :].bitcast(I32))
+
+        def load_words(k):
             nc.sync.dma_start(out=key_words[k][:, :U],
                               in_=words_in[k][0].rearrange("p n t -> p (n t)").bitcast(I32))
+
+        nc.sync.dma_start(lists[0][:], lists_in[0])
+        load_scales(0, nc.scalar)
+        load_words(0)
+        for k in (1, 2):
+            nc.sync.dma_start(lists[k][:], lists_in[k])
+            load_words(k)
         q_raw = keep.tile([P, PACK, Q], F32)
         nc.sync.dma_start(out=q_raw[:], in_=query.rearrange("(p j) w -> p j w", j=PACK))
+        for k in (1, 2):
+            load_scales(k, nc.sync)
+        last = E_TILES - 1
         for k in books:
-            for quad in range(4):
-                nc.sync.dma_start(out=key_scales[k][32 * quad:32 * quad + 4, :U].bitcast(I32),
-                                  in_=scales_in[k][0, 4 * quad:4 * quad + 4, :].bitcast(I32))
+            load_values(k, last)
 
         factor_rows = keep.tile([P, P], F32)
         nc.gpsimd.memset(factor_rows[:], 0.0)
@@ -105,32 +114,24 @@ def tile_attend_additivekeys_kernel(tc, query, ba_words, ba_scales, bb_words, bb
                                      is_transpose=True, start=(k == 0 and t == 0), stop=(k == 2 and t == PACK - 1))
             return bank
 
-        def scale_on_scalar(bank, first, name):
-            woven = keep.tile([P, P, PACK], BF16, name=name, align_bytes=64)
+        early = keep.tile([P, E_TILES, P, PACK], BF16, align_bytes=64)
+
+        def scale_on_scalar(bank, first, place):
             for t in range(PACK):
-                nc.scalar.activation(out=woven[:, :, t], in_=bank[:, t * P:(t + 1) * P], func=ACT.Copy,
+                nc.scalar.activation(out=early[:, place, :, t], in_=bank[:, t * P:(t + 1) * P], func=ACT.Copy,
                                      scale=factors[:, first + t:first + t + 1])
-            return woven
-
-        def quantise(woven, name):
-            codes = keep.tile([P, P], U32, name=name + "_codes", align_bytes=64)
-            plane = keep.tile([P, P], U8, name=name + "_plane", align_bytes=64)
-            nc.vector.quantize_mx(out=codes[:].bitcast(FP8X4), scales=plane[:],
-                                  in_=woven[:].rearrange("p x t -> p (x t)"))
-            return codes, plane
-
-        banks = {last: gather_values(last)}
-        woven_v = {last: scale_on_scalar(banks[last], 0, "vv%d" % last)}
 
         picked_words = [keep.tile([P, I], U32, name="picked_words%d" % k, align_bytes=64) for k in books]
         picked_scales = [keep.tile([P, I], U8, name="picked_scales%d" % k, align_bytes=64) for k in books]
+        nc.vector.tensor_copy(out=picked_scales[0][:], in_=key_scales[0][:].indirect(lists[0][:]))
         for k in books:
             nc.vector.tensor_copy(out=picked_words[k][:], in_=key_words[k][:].bitcast(U32).indirect(lists[k][:]))
         nc.vector.quantize_mx(out=q_codes[:].bitcast(FP8X4), scales=q_scale[:],
                               in_=q_bf[:].rearrange("p w j -> p (w j)"))
+        for k in (1, 2):
+            nc.vector.tensor_copy(out=picked_scales[k][:], in_=key_scales[k][:].indirect(lists[k][:]))
         scores = psum.tile([P, I], F32)
         for k in books:
-            nc.vector.tensor_copy(out=picked_scales[k][:], in_=key_scales[k][:].indirect(lists[k][:]))
             nc.tensor.matmul_mx(out=scores[:], lhsT=q_codes[:].bitcast(FP8X4), lhsT_scale=q_scale[:],
                                 rhs=picked_words[k][:].bitcast(FP8X4), rhs_scale=picked_scales[k][:],
                                 start=(k == 0), stop=(k == 2))
@@ -149,23 +150,38 @@ def tile_attend_additivekeys_kernel(tc, query, ba_words, ba_scales, bb_words, bb
         weight_bank = psum.tile([P, PACK * P], F32)
         for t in range(PACK):
             nc.tensor.transpose(weight_bank[:, t * P:(t + 1) * P], prob_dealt[:, t * P:(t + 1) * P], ident[:])
-        w_codes, w_plane = quantise(scale_on_scalar(weight_bank, PACK, "wt"), "wt")
+        scale_on_scalar(weight_bank, PACK, 0)
 
-        def finish(g, woven):
-            codes, plane = quantise(woven, "vv%d" % g)
-            result_bank = psum2.tile([P, P], F32, name="result_bank")
-            nc.tensor.matmul_mx(out=result_bank[:], lhsT=w_codes[:].bitcast(FP8X4), lhsT_scale=w_plane[:],
-                                rhs=codes[:].bitcast(FP8X4), rhs_scale=plane[:], start=True, stop=True)
-            result = ring.tile([P, P], F32, name="result")
-            nc.scalar.copy(out=result[:], in_=result_bank[:])
-            nc.sync.dma_start(out=out[:, g * P:(g + 1) * P], in_=result[:])
-
-        finish(last, woven_v[last])
-        for g in reversed(range(1, last)):
-            finish(g, scale_on_scalar(gather_values(g), 0, "vv%d" % g))
+        for g in reversed(range(1, E_TILES)):
+            scale_on_scalar(gather_values(g), 0, g)
         bank = gather_values(0)
-        woven = keep.tile([P, P, PACK], BF16, name="vv0", align_bytes=64)
+
+        early_codes = keep.tile([P, E_TILES * P], U32, name="early_codes", tag="table2", align_bytes=64)
+        early_plane = keep.tile([P, E_TILES * P], U8, align_bytes=64)
+        nc.vector.quantize_mx(out=early_codes[:].bitcast(FP8X4), scales=early_plane[:],
+                              in_=early[:].rearrange("p g x t -> p (g x t)"))
+
+        def product(result_bank, codes, plane):
+            nc.tensor.matmul_mx(out=result_bank, lhsT=early_codes[:, :P].bitcast(FP8X4), lhsT_scale=early_plane[:, :P],
+                                rhs=codes.bitcast(FP8X4), rhs_scale=plane, start=True, stop=True)
+
+        early_bank = psum.tile([P, E], F32)
+        for lo, hi in ((P, 2 * P), (2 * P, E)):
+            product(early_bank[:, lo:hi], early_codes[:, lo:hi], early_plane[:, lo:hi])
+        early_result = keep.tile([P, E - P], F32)
+        nc.scalar.copy(out=early_result[:], in_=early_bank[:, P:])
+        nc.sync.dma_start(out=out[:, P:], in_=early_result[:])
+
+        woven = keep.tile([P, P, PACK], BF16, align_bytes=64)
         nc.vector.tensor_tensor(out=woven[:], in0=bank[:].rearrange("p (t e) -> p e t", t=PACK),
                                 in1=factors[:, 0:PACK].rearrange("p (o t) -> p o t", o=1).to_broadcast([P, P, PACK]),
                                 op=ALU.mult)
-        finish(0, woven)
+        late_codes = keep.tile([P, P], U32, align_bytes=64)
+        late_plane = keep.tile([P, P], U8, align_bytes=64)
+        nc.vector.quantize_mx(out=late_codes[:].bitcast(FP8X4), scales=late_plane[:],
+                              in_=woven[:].rearrange("p x t -> p (x t)"))
+        late_bank = psum.tile([P, P], F32)
+        product(late_bank[:], late_codes[:], late_plane[:])
+        late_result = keep.tile([P, P], F32)
+        nc.scalar.copy(out=late_result[:], in_=late_bank[:])
+        nc.sync.dma_start(out=out[:, :P], in_=late_result[:])

@@ -45,19 +45,24 @@ def tile_attend_additivekeys_kernel(tc, query, ba_words, ba_scales, bb_words, bb
         key_scales = [keep.tile([P, WINDOW], U8, name="key_scales%d" % k) for k in books]
         tables = [keep.tile([P, E_TILES * U + SPARE], F32, name="table%d" % k, tag="table%d" % k, align_bytes=64) for k in books]
 
-        for k in books:
-            nc.gpsimd.memset(key_scales[k][:].bitcast(I32), 0)
+        first_row = P - BLOCKS
+        nc.vector.memset(key_scales[0][:first_row, :U].bitcast(I32), 0)
+        nc.vector.memset(key_scales[0][:, U:].bitcast(I32), 0)
         for k in books:
             nc.vector.memset(key_words[k][:, U:], 0)
+        for k in (1, 2):
+            nc.gpsimd.memset(key_scales[k][:].bitcast(I32), 0)
+        first_plane = keep.tile([P, I], U8, align_bytes=64)
+        nc.gpsimd.memset(first_plane[:].bitcast(I32), 0)
         for k in books:
-            nc.vector.memset(tables[k][:, E_TILES * U:], 0.0)
+            nc.gpsimd.memset(tables[k][:, E_TILES * U:], 0.0)
 
         def load_values(k, g):
             nc.sync.dma_start(out=tables[k][:, g * U:(g + 1) * U], in_=values_in[k][g * P:(g + 1) * P, :])
 
-        def load_scales(k, queue):
+        def load_scales(k):
             for quad in range(4):
-                queue.dma_start(out=key_scales[k][32 * quad:32 * quad + 4, :U].bitcast(I32),
+                nc.sync.dma_start(out=key_scales[k][32 * quad:32 * quad + 4, :U].bitcast(I32),
                                   in_=scales_in[k][0, 4 * quad:4 * quad + 4, :].bitcast(I32))
 
         def load_words(k):
@@ -65,15 +70,20 @@ def tile_attend_additivekeys_kernel(tc, query, ba_words, ba_scales, bb_words, bb
                               in_=words_in[k][0].rearrange("p n t -> p (n t)").bitcast(I32))
 
         nc.sync.dma_start(lists[0][:], lists_in[0])
-        load_scales(0, nc.scalar)
+        nc.sync.dma_start(out=key_scales[0][first_row:, :U].bitcast(I32), in_=scales_in[0][0].bitcast(I32))
         load_words(0)
         for k in (1, 2):
             nc.sync.dma_start(lists[k][:], lists_in[k])
             load_words(k)
         q_raw = keep.tile([P, PACK, Q], F32)
         nc.sync.dma_start(out=q_raw[:], in_=query.rearrange("(p j) w -> p j w", j=PACK))
+        picked_scales = [keep.tile([P, I], U8, name="picked_scales%d" % k, align_bytes=64) for k in books]
+        nc.vector.tensor_copy(out=picked_scales[0][:], in_=key_scales[0][:].indirect(lists[0][:]))
+        for quad in range(4):
+            nc.sync.dma_start(out=first_plane[32 * quad:32 * quad + 4, :].bitcast(I32),
+                              in_=picked_scales[0][first_row + 4 * quad:first_row + 4 * quad + 4, :].bitcast(I32))
         for k in (1, 2):
-            load_scales(k, nc.sync)
+            load_scales(k)
         last = E_TILES - 1
         for k in books:
             load_values(k, last)
@@ -91,7 +101,7 @@ def tile_attend_additivekeys_kernel(tc, query, ba_words, ba_scales, bb_words, bb
         ident = keep.tile([P, P], F32)
         make_identity(nc, ident[:])
 
-        factor_bank = psum.tile([P, P], F32)
+        factor_bank = psum.tile([P, P], F32, tag="narrow_bank")
         nc.tensor.transpose(factor_bank[:], factor_rows[:], ident[:])
         factors = keep.tile([P, 2 * PACK], F32)
         nc.scalar.copy(out=factors[:], in_=factor_bank[:, :2 * PACK])
@@ -122,18 +132,17 @@ def tile_attend_additivekeys_kernel(tc, query, ba_words, ba_scales, bb_words, bb
                                      scale=factors[:, first + t:first + t + 1])
 
         picked_words = [keep.tile([P, I], U32, name="picked_words%d" % k, align_bytes=64) for k in books]
-        picked_scales = [keep.tile([P, I], U8, name="picked_scales%d" % k, align_bytes=64) for k in books]
-        nc.vector.tensor_copy(out=picked_scales[0][:], in_=key_scales[0][:].indirect(lists[0][:]))
         for k in books:
             nc.vector.tensor_copy(out=picked_words[k][:], in_=key_words[k][:].bitcast(U32).indirect(lists[k][:]))
         nc.vector.quantize_mx(out=q_codes[:].bitcast(FP8X4), scales=q_scale[:],
                               in_=q_bf[:].rearrange("p w j -> p (w j)"))
         for k in (1, 2):
             nc.vector.tensor_copy(out=picked_scales[k][:], in_=key_scales[k][:].indirect(lists[k][:]))
+        key_planes = (first_plane, picked_scales[1], picked_scales[2])
         scores = psum.tile([P, I], F32)
         for k in books:
             nc.tensor.matmul_mx(out=scores[:], lhsT=q_codes[:].bitcast(FP8X4), lhsT_scale=q_scale[:],
-                                rhs=picked_words[k][:].bitcast(FP8X4), rhs_scale=picked_scales[k][:],
+                                rhs=picked_words[k][:].bitcast(FP8X4), rhs_scale=key_planes[k][:],
                                 start=(k == 0), stop=(k == 2))
 
         neg_max = keep.tile([P, 1], F32)
@@ -165,23 +174,29 @@ def tile_attend_additivekeys_kernel(tc, query, ba_words, ba_scales, bb_words, bb
             nc.tensor.matmul_mx(out=result_bank, lhsT=early_codes[:, :P].bitcast(FP8X4), lhsT_scale=early_plane[:, :P],
                                 rhs=codes.bitcast(FP8X4), rhs_scale=plane, start=True, stop=True)
 
-        early_bank = psum.tile([P, E], F32)
-        for lo, hi in ((P, 2 * P), (2 * P, E)):
-            product(early_bank[:, lo:hi], early_codes[:, lo:hi], early_plane[:, lo:hi])
-        early_result = keep.tile([P, E - P], F32)
-        nc.scalar.copy(out=early_result[:], in_=early_bank[:, P:])
-        nc.sync.dma_start(out=out[:, P:], in_=early_result[:])
+        for lo, hi, tag in ((2 * P, E, "wide_bank"), (P, 2 * P, "narrow_bank")):
+            early_bank = psum.tile([P, hi - lo], F32, name="early_" + tag, tag=tag)
+            product(early_bank[:], early_codes[:, lo:hi], early_plane[:, lo:hi])
+            early_result = keep.tile([P, hi - lo], F32, name="result_" + tag)
+            nc.scalar.copy(out=early_result[:], in_=early_bank[:])
+            nc.sync.dma_start(out=out[:, lo:hi], in_=early_result[:])
 
-        woven = keep.tile([P, P, PACK], BF16, align_bytes=64)
-        nc.vector.tensor_tensor(out=woven[:], in0=bank[:].rearrange("p (t e) -> p e t", t=PACK),
-                                in1=factors[:, 0:PACK].rearrange("p (o t) -> p o t", o=1).to_broadcast([P, P, PACK]),
-                                op=ALU.mult)
-        late_codes = keep.tile([P, P], U32, align_bytes=64)
-        late_plane = keep.tile([P, P], U8, align_bytes=64)
-        nc.vector.quantize_mx(out=late_codes[:].bitcast(FP8X4), scales=late_plane[:],
-                              in_=woven[:].rearrange("p x t -> p (x t)"))
-        late_bank = psum.tile([P, P], F32)
-        product(late_bank[:], late_codes[:], late_plane[:])
+        half = P // 2
+        halves = range(2)
+        woven = [keep.tile([P, half, PACK], BF16, name="woven%d" % h, align_bytes=64) for h in halves]
+        late_codes = [keep.tile([P, half], U32, name="late_codes%d" % h, align_bytes=64) for h in halves]
+        late_plane = [keep.tile([P, half], U8, name="late_plane%d" % h, align_bytes=64) for h in halves]
+        late_bank = [psum.tile([P, half], F32, name="late_bank%d" % h) for h in halves]
         late_result = keep.tile([P, P], F32)
-        nc.scalar.copy(out=late_result[:], in_=late_bank[:])
+        for h in halves:
+            nc.vector.tensor_tensor(
+                out=woven[h][:], in0=bank[:].rearrange("p (t e) -> p e t", t=PACK)[:, h * half:(h + 1) * half, :],
+                in1=factors[:, 0:PACK].rearrange("p (o t) -> p o t", o=1).to_broadcast([P, half, PACK]),
+                op=ALU.mult)
+        for h in halves:
+            nc.vector.quantize_mx(out=late_codes[h][:].bitcast(FP8X4), scales=late_plane[h][:],
+                                  in_=woven[h][:].rearrange("p x t -> p (x t)"))
+            product(late_bank[h][:], late_codes[h][:], late_plane[h][:])
+        nc.scalar.copy(out=late_result[:, :half], in_=late_bank[0][:])
+        nc.vector.tensor_copy(out=late_result[:, half:], in_=late_bank[1][:])
         nc.sync.dma_start(out=out[:, :P], in_=late_result[:])

@@ -48,14 +48,15 @@ def tile_attend_additivekeys_kernel(tc, query, ba_words, ba_scales, bb_words, bb
         first_row = P - BLOCKS
         nc.vector.memset(key_scales[0][:first_row, :U].bitcast(I32), 0)
         nc.vector.memset(key_scales[0][:, U:].bitcast(I32), 0)
-        for k in books:
-            nc.vector.memset(key_words[k][:, U:], 0)
+        nc.vector.memset(key_words[0][:, U:], 0)
         for k in (1, 2):
-            nc.gpsimd.memset(key_scales[k][:].bitcast(I32), 0)
+            nc.vector.memset(key_scales[k][:].bitcast(I32), 0)
+        for k in (1, 2):
+            nc.vector.memset(key_words[k][:, U:], 0)
         first_plane = keep.tile([P, I], U8, align_bytes=64)
-        nc.gpsimd.memset(first_plane[:].bitcast(I32), 0)
+        nc.vector.memset(first_plane[:].bitcast(I32), 0)
         for k in books:
-            nc.gpsimd.memset(tables[k][:, E_TILES * U:], 0.0)
+            nc.vector.memset(tables[k][:, E_TILES * U:], 0.0)
 
         def load_values(k, g):
             nc.sync.dma_start(out=tables[k][:, g * U:(g + 1) * U], in_=values_in[k][g * P:(g + 1) * P, :])
@@ -167,8 +168,10 @@ def tile_attend_additivekeys_kernel(tc, query, ba_words, ba_scales, bb_words, bb
 
         early_codes = keep.tile([P, E_TILES * P], U32, name="early_codes", tag="table2", align_bytes=64)
         early_plane = keep.tile([P, E_TILES * P], U8, align_bytes=64)
-        nc.vector.quantize_mx(out=early_codes[:].bitcast(FP8X4), scales=early_plane[:],
-                              in_=early[:].rearrange("p g x t -> p (g x t)"))
+        for lo in (2, 0):
+            nc.vector.quantize_mx(out=early_codes[:, lo * P:(lo + 2) * P].bitcast(FP8X4),
+                                  scales=early_plane[:, lo * P:(lo + 2) * P],
+                                  in_=early[:, lo:lo + 2].rearrange("p g x t -> p (g x t)"))
 
         def product(result_bank, codes, plane):
             nc.tensor.matmul_mx(out=result_bank, lhsT=early_codes[:, :P].bitcast(FP8X4), lhsT_scale=early_plane[:, :P],

@@ -20,7 +20,7 @@ P = 128
 PACK = 4
 RUN = 8
 BLOCKS = 16
-SPARE = 192
+SPARE = 176
 WINDOW = U + SPARE
 E_TILES = E // P
 
@@ -90,7 +90,7 @@ def tile_attend_additivekeys_kernel(tc, query, ba_words, ba_scales, bb_words, bb
             load_values(k, last)
 
         factor_rows = keep.tile([P, P], F32)
-        nc.gpsimd.memset(factor_rows[:], 0.0)
+        nc.vector.memset(factor_rows[:], 0.0)
         nc.sync.dma_start(out=factor_rows[0:PACK, :].rearrange("t (b j) -> t b j", j=RUN),
                           in_=vsc.rearrange("(b t j) o -> t b (j o)", t=PACK, j=RUN))
         nc.sync.dma_start(out=factor_rows[PACK:2 * PACK, :].rearrange("t (b j) -> t b j", j=RUN),
@@ -128,9 +128,11 @@ def tile_attend_additivekeys_kernel(tc, query, ba_words, ba_scales, bb_words, bb
         early = keep.tile([P, E_TILES, P, PACK], BF16, align_bytes=64)
 
         def scale_on_scalar(bank, first, place):
+            scaled = ring.tile([P, PACK, P], BF16)
             for t in range(PACK):
-                nc.scalar.activation(out=early[:, place, :, t], in_=bank[:, t * P:(t + 1) * P], func=ACT.Copy,
+                nc.scalar.activation(out=scaled[:, t, :], in_=bank[:, t * P:(t + 1) * P], func=ACT.Copy,
                                      scale=factors[:, first + t:first + t + 1])
+            nc.scalar.copy(out=early[:, place], in_=scaled[:].rearrange("p t x -> p x t"))
 
         picked_words = [keep.tile([P, I], U32, name="picked_words%d" % k, align_bytes=64) for k in books]
         for k in books:
@@ -168,10 +170,10 @@ def tile_attend_additivekeys_kernel(tc, query, ba_words, ba_scales, bb_words, bb
 
         early_codes = keep.tile([P, E_TILES * P], U32, name="early_codes", tag="table2", align_bytes=64)
         early_plane = keep.tile([P, E_TILES * P], U8, align_bytes=64)
-        for lo in (2, 0):
-            nc.vector.quantize_mx(out=early_codes[:, lo * P:(lo + 2) * P].bitcast(FP8X4),
-                                  scales=early_plane[:, lo * P:(lo + 2) * P],
-                                  in_=early[:, lo:lo + 2].rearrange("p g x t -> p (g x t)"))
+        for lo, hi in ((2, 4), (0, 1), (1, 2)):
+            nc.vector.quantize_mx(out=early_codes[:, lo * P:hi * P].bitcast(FP8X4),
+                                  scales=early_plane[:, lo * P:hi * P],
+                                  in_=early[:, lo:hi].rearrange("p g x t -> p (g x t)"))
 
         def product(result_bank, codes, plane):
             nc.tensor.matmul_mx(out=result_bank, lhsT=early_codes[:, :P].bitcast(FP8X4), lhsT_scale=early_plane[:, :P],

@@ -41,22 +41,24 @@ def tile_attend_additivekeys_kernel(tc, query, ba_words, ba_scales, bb_words, bb
         psum2 = ctx.enter_context(tc.psum_pool(name="psum2", bufs=2))
 
         lists = [keep.tile([P, I // 16], U16, name="list%d" % k) for k in books]
-        key_words = [keep.tile([P, WINDOW], I32, name="key_words%d" % k) for k in books]
-        key_scales = [keep.tile([P, WINDOW], U8, name="key_scales%d" % k) for k in books]
+        key_words = [keep.tile([P, WINDOW + 1], I32, name="key_words%d" % k) for k in books]
+        key_scales = [keep.tile([P, WINDOW + 4], U8, name="key_scales%d" % k, tag="key_scales%d" % k, align_bytes=64)
+                      for k in books]
         tables = [keep.tile([P, E_TILES * U + SPARE], F32, name="table%d" % k, tag="table%d" % k, align_bytes=64) for k in books]
 
+        ident = keep.tile([P, P], F32)
+        make_identity(nc, ident[:])
+
         first_row = P - BLOCKS
-        nc.vector.memset(key_scales[0][:first_row, :U].bitcast(I32), 0)
+        nc.vector.memset(key_scales[0][:first_row, :U + 4].bitcast(I32), 0)
         nc.vector.memset(key_scales[0][:, U:].bitcast(I32), 0)
         nc.vector.memset(key_words[0][:, U:], 0)
-        for k in (1, 2):
-            nc.vector.memset(key_scales[k][:].bitcast(I32), 0)
+        nc.vector.memset(key_scales[1][:].bitcast(I32), 0)
         for k in (1, 2):
             nc.vector.memset(key_words[k][:, U:], 0)
-        first_plane = keep.tile([P, I], U8, align_bytes=64)
-        nc.vector.memset(first_plane[:].bitcast(I32), 0)
+        nc.gpsimd.memset(key_scales[2][:].bitcast(I32), 0)
         for k in books:
-            nc.vector.memset(tables[k][:, E_TILES * U:], 0.0)
+            nc.gpsimd.memset(tables[k][:, E_TILES * U:], 0.0)
 
         def load_values(k, g):
             nc.sync.dma_start(out=tables[k][:, g * U:(g + 1) * U], in_=values_in[k][g * P:(g + 1) * P, :])
@@ -79,36 +81,30 @@ def tile_attend_additivekeys_kernel(tc, query, ba_words, ba_scales, bb_words, bb
         q_raw = keep.tile([P, PACK, Q], F32)
         nc.sync.dma_start(out=q_raw[:], in_=query.rearrange("(p j) w -> p j w", j=PACK))
         picked_scales = [keep.tile([P, I], U8, name="picked_scales%d" % k, align_bytes=64) for k in books]
-        nc.vector.tensor_copy(out=picked_scales[0][:], in_=key_scales[0][:].indirect(lists[0][:]))
-        for quad in range(4):
-            nc.sync.dma_start(out=first_plane[32 * quad:32 * quad + 4, :].bitcast(I32),
-                              in_=picked_scales[0][first_row + 4 * quad:first_row + 4 * quad + 4, :].bitcast(I32))
+        nc.vector.tensor_copy(out=picked_scales[0][:], in_=key_scales[0][:, :WINDOW].indirect(lists[0][:]))
         for k in (1, 2):
             load_scales(k)
         last = E_TILES - 1
+        first_plane = keep.tile([P, I], U8, name="first_plane", tag="key_scales0", align_bytes=64)
+        for quad in range(4):
+            nc.sync.dma_start(out=first_plane[32 * quad:32 * quad + 4, :].bitcast(I32),
+                              in_=picked_scales[0][first_row + 4 * quad:first_row + 4 * quad + 4, :].bitcast(I32))
         for k in books:
             load_values(k, last)
 
-        factor_rows = keep.tile([P, P], F32)
-        nc.vector.memset(factor_rows[:], 0.0)
+        q_bf = keep.tile([P, Q, PACK], BF16, align_bytes=64)
+        nc.scalar.copy(out=q_bf[:], in_=q_raw[:].rearrange("p j w -> p w j"))
+        factor_rows = q_raw[:, 0, :]
         nc.sync.dma_start(out=factor_rows[0:PACK, :].rearrange("t (b j) -> t b j", j=RUN),
-                          in_=vsc.rearrange("(b t j) o -> t b (j o)", t=PACK, j=RUN))
+                            in_=vsc.rearrange("(b t j) o -> t b (j o)", t=PACK, j=RUN))
         nc.sync.dma_start(out=factor_rows[PACK:2 * PACK, :].rearrange("t (b j) -> t b j", j=RUN),
-                          in_=size.rearrange("o (b t j) -> (o t) b j", t=PACK, j=RUN))
+                            in_=size.rearrange("o (b t j) -> (o t) b j", t=PACK, j=RUN))
         for g in reversed(range(last)):
             for k in books:
                 load_values(k, g)
 
-        ident = keep.tile([P, P], F32)
-        make_identity(nc, ident[:])
-
-        factor_bank = psum.tile([P, P], F32, tag="narrow_bank")
-        nc.tensor.transpose(factor_bank[:], factor_rows[:], ident[:])
         factors = keep.tile([P, 2 * PACK], F32)
-        nc.scalar.copy(out=factors[:], in_=factor_bank[:, :2 * PACK])
 
-        q_bf = keep.tile([P, Q, PACK], BF16, align_bytes=64)
-        nc.scalar.copy(out=q_bf[:], in_=q_raw[:].rearrange("p j w -> p w j"))
         q_codes = keep.tile([P, Q], U32, align_bytes=64)
         q_scale = keep.tile([P, Q], U8, align_bytes=64)
 
@@ -136,11 +132,11 @@ def tile_attend_additivekeys_kernel(tc, query, ba_words, ba_scales, bb_words, bb
 
         picked_words = [keep.tile([P, I], U32, name="picked_words%d" % k, align_bytes=64) for k in books]
         for k in books:
-            nc.vector.tensor_copy(out=picked_words[k][:], in_=key_words[k][:].bitcast(U32).indirect(lists[k][:]))
+            nc.vector.tensor_copy(out=picked_words[k][:], in_=key_words[k][:, :WINDOW].bitcast(U32).indirect(lists[k][:]))
         nc.vector.quantize_mx(out=q_codes[:].bitcast(FP8X4), scales=q_scale[:],
                               in_=q_bf[:].rearrange("p w j -> p (w j)"))
         for k in (1, 2):
-            nc.vector.tensor_copy(out=picked_scales[k][:], in_=key_scales[k][:].indirect(lists[k][:]))
+            nc.vector.tensor_copy(out=picked_scales[k][:], in_=key_scales[k][:, :WINDOW].indirect(lists[k][:]))
         key_planes = (first_plane, picked_scales[1], picked_scales[2])
         scores = psum.tile([P, I], F32)
         for k in books:
@@ -159,6 +155,9 @@ def tile_attend_additivekeys_kernel(tc, query, ba_words, ba_scales, bb_words, bb
         nc.scalar.activation(out=prob_dealt[:].rearrange("p (t b j) -> p t b j", t=PACK, j=RUN),
                              in_=prob[:].rearrange("p (b t j) -> p t b j", t=PACK, j=RUN),
                              func=ACT.Copy, scale=inv_sum[:])
+        factor_bank = psum.tile([P, P], F32, tag="narrow_bank")
+        nc.tensor.transpose(factor_bank[:], factor_rows, ident[:])
+        nc.scalar.copy(out=factors[:], in_=factor_bank[:, :2 * PACK])
         weight_bank = psum.tile([P, PACK * P], F32)
         for t in range(PACK):
             nc.tensor.transpose(weight_bank[:, t * P:(t + 1) * P], prob_dealt[:, t * P:(t + 1) * P], ident[:])

@@ -108,8 +108,7 @@ def tile_attend_additivekeys_kernel(tc, query, ba_words, ba_scales, bb_words, bb
         q_codes = keep.tile([P, Q], U32, align_bytes=64)
         q_scale = keep.tile([P, Q], U8, align_bytes=64)
 
-        def gather_values(g):
-            bank = psum2.tile([P, PACK * P], F32, name="value_bank")
+        def gather_values(g, places):
             for k in books:
                 picked = ring.tile([P, I], F32, name="picked%d" % k)
                 window = tables[k][:, g * U:g * U + WINDOW].bitcast(U32)
@@ -117,9 +116,9 @@ def tile_attend_additivekeys_kernel(tc, query, ba_words, ba_scales, bb_words, bb
                     out=picked[:].bitcast(U32).rearrange("p (t b j) -> p b t j", t=PACK, j=RUN),
                     in_=window.indirect(lists[k][:]))
                 for t in range(PACK):
-                    nc.tensor.matmul(bank[:, t * P:(t + 1) * P], lhsT=picked[:, t * P:(t + 1) * P], rhs=ident[:],
-                                     is_transpose=True, start=(k == 0 and t == 0), stop=(k == 2 and t == PACK - 1))
-            return bank
+                    region, opens, closes = places[t]
+                    nc.tensor.matmul(region, lhsT=picked[:, t * P:(t + 1) * P], rhs=ident[:],
+                                     is_transpose=True, start=(k == 0 and opens), stop=(k == 2 and closes))
 
         early = keep.tile([P, E_TILES, P, PACK], BF16, align_bytes=64)
 
@@ -138,7 +137,7 @@ def tile_attend_additivekeys_kernel(tc, query, ba_words, ba_scales, bb_words, bb
         for k in (1, 2):
             nc.vector.tensor_copy(out=picked_scales[k][:], in_=key_scales[k][:, :WINDOW].indirect(lists[k][:]))
         key_planes = (first_plane, picked_scales[1], picked_scales[2])
-        scores = psum.tile([P, I], F32)
+        scores = psum.tile([P, I], F32, name="scores", tag="scores")
         for k in books:
             nc.tensor.matmul_mx(out=scores[:], lhsT=q_codes[:].bitcast(FP8X4), lhsT_scale=q_scale[:],
                                 rhs=picked_words[k][:].bitcast(FP8X4), rhs_scale=key_planes[k][:],
@@ -158,14 +157,20 @@ def tile_attend_additivekeys_kernel(tc, query, ba_words, ba_scales, bb_words, bb
         factor_bank = psum.tile([P, P], F32, tag="narrow_bank")
         nc.tensor.transpose(factor_bank[:], factor_rows, ident[:])
         nc.scalar.copy(out=factors[:], in_=factor_bank[:, :2 * PACK])
-        weight_bank = psum.tile([P, PACK * P], F32)
+        weight_bank = psum.tile([P, PACK * P], F32, name="weight_bank", tag="weight_bank")
         for t in range(PACK):
             nc.tensor.transpose(weight_bank[:, t * P:(t + 1) * P], prob_dealt[:, t * P:(t + 1) * P], ident[:])
         scale_on_scalar(weight_bank, PACK, 0)
 
         for g in reversed(range(1, E_TILES)):
-            scale_on_scalar(gather_values(g), 0, g)
-        bank = gather_values(0)
+            bank = psum2.tile([P, PACK * P], F32, name="value_bank")
+            gather_values(g, [(bank[:, t * P:(t + 1) * P], t == 0, t == PACK - 1) for t in range(PACK)])
+            scale_on_scalar(bank, 0, g)
+        place0 = psum.tile([P, P], F32, name="place0", tag="scores")
+        place1 = psum.tile([P, P], F32, name="place1", tag="weight_bank")
+        pair = psum2.tile([P, 2 * P], F32, name="pair", tag="value_bank")
+        gather_values(0, [(place0[:], True, True), (place1[:], True, True),
+                          (pair[:, :P], True, False), (pair[:, P:], False, True)])
 
         early_codes = keep.tile([P, E_TILES * P], U32, name="early_codes", tag="table2", align_bytes=64)
         early_plane = keep.tile([P, E_TILES * P], U8, align_bytes=64)
@@ -178,6 +183,14 @@ def tile_attend_additivekeys_kernel(tc, query, ba_words, ba_scales, bb_words, bb
             nc.tensor.matmul_mx(out=result_bank, lhsT=early_codes[:, :P].bitcast(FP8X4), lhsT_scale=early_plane[:, :P],
                                 rhs=codes.bitcast(FP8X4), rhs_scale=plane, start=True, stop=True)
 
+        half = P // 2
+        halves = range(2)
+        woven = [keep.tile([P, half, PACK], BF16, name="woven%d" % h, align_bytes=64) for h in halves]
+        for h in halves:
+            for t, place in enumerate((place0, place1)):
+                nc.scalar.activation(out=woven[h][:, :, t], in_=place[:, h * half:(h + 1) * half], func=ACT.Copy,
+                                     scale=factors[:, t:t + 1])
+
         for lo, hi, tag in ((2 * P, E, "wide_bank"), (P, 2 * P, "narrow_bank")):
             early_bank = psum.tile([P, hi - lo], F32, name="early_" + tag, tag=tag)
             product(early_bank[:], early_codes[:, lo:hi], early_plane[:, lo:hi])
@@ -185,17 +198,14 @@ def tile_attend_additivekeys_kernel(tc, query, ba_words, ba_scales, bb_words, bb
             nc.scalar.copy(out=early_result[:], in_=early_bank[:])
             nc.sync.dma_start(out=out[:, lo:hi], in_=early_result[:])
 
-        half = P // 2
-        halves = range(2)
-        woven = [keep.tile([P, half, PACK], BF16, name="woven%d" % h, align_bytes=64) for h in halves]
         late_codes = [keep.tile([P, half], U32, name="late_codes%d" % h, align_bytes=64) for h in halves]
         late_plane = [keep.tile([P, half], U8, name="late_plane%d" % h, align_bytes=64) for h in halves]
         late_bank = [psum.tile([P, half], F32, name="late_bank%d" % h) for h in halves]
         late_result = keep.tile([P, P], F32)
         for h in halves:
             nc.vector.tensor_tensor(
-                out=woven[h][:], in0=bank[:].rearrange("p (t e) -> p e t", t=PACK)[:, h * half:(h + 1) * half, :],
-                in1=factors[:, 0:PACK].rearrange("p (o t) -> p o t", o=1).to_broadcast([P, half, PACK]),
+                out=woven[h][:, :, 2:], in0=pair[:].rearrange("p (t e) -> p e t", t=2)[:, h * half:(h + 1) * half, :],
+                in1=factors[:, 2:PACK].rearrange("p (o t) -> p o t", o=1).to_broadcast([P, half, 2]),
                 op=ALU.mult)
         for h in halves:
             nc.vector.quantize_mx(out=late_codes[h][:].bitcast(FP8X4), scales=late_plane[h][:],

@@ -37,6 +37,7 @@ def tile_attend_additivekeys_kernel(tc, query, ba_words, ba_scales, bb_words, bb
     with ExitStack() as ctx:
         keep = ctx.enter_context(tc.tile_pool(name="keep", bufs=1))
         ring = ctx.enter_context(tc.tile_pool(name="ring", bufs=2))
+        shared = ctx.enter_context(tc.tile_pool(name="shared", bufs=1))
         psum = ctx.enter_context(tc.psum_pool(name="psum", bufs=1))
         psum2 = ctx.enter_context(tc.psum_pool(name="psum2", bufs=2))
 
@@ -185,7 +186,7 @@ def tile_attend_additivekeys_kernel(tc, query, ba_words, ba_scales, bb_words, bb
 
         half = P // 2
         halves = range(2)
-        woven = [keep.tile([P, half, PACK], BF16, name="woven%d" % h, align_bytes=64) for h in halves]
+        woven = [shared.tile([P, half, PACK], BF16, name="woven%d" % h, align_bytes=64) for h in halves]
         for h in halves:
             for t, place in enumerate((place0, place1)):
                 nc.scalar.activation(out=woven[h][:, :, t], in_=place[:, h * half:(h + 1) * half], func=ACT.Copy,
@@ -194,7 +195,7 @@ def tile_attend_additivekeys_kernel(tc, query, ba_words, ba_scales, bb_words, bb
         for lo, hi, tag in ((2 * P, E, "wide_bank"), (P, 2 * P, "narrow_bank")):
             early_bank = psum.tile([P, hi - lo], F32, name="early_" + tag, tag=tag)
             product(early_bank[:], early_codes[:, lo:hi], early_plane[:, lo:hi])
-            early_result = keep.tile([P, hi - lo], F32, name="result_" + tag)
+            early_result = (keep if hi - lo > P else shared).tile([P, hi - lo], F32, name="result_" + tag)
             nc.scalar.copy(out=early_result[:], in_=early_bank[:])
             nc.sync.dma_start(out=out[:, lo:hi], in_=early_result[:])
 

@@ -18,200 +18,209 @@ ALU = mybir.AluOpType
 
 P = 128
 PACK = 4
-RUN = 8
 BLOCKS = 16
-SPARE = 176
-WINDOW = U + SPARE
 E_TILES = E // P
+WORD_WINDOW = U + 177
+BYTE_WINDOW = U + 180
+FLOAT_WINDOW = U + 8
 
 
 def tile_attend_additivekeys_kernel(tc, query, ba_words, ba_scales, bb_words, bb_scales, bc_words, bc_scales,
-                                     size, ca, cb, cc, vsc, offs, offs2, offs3, out):
+                                         size, ca, cb, cc, vsc, offs, offs2, offs3, out):
     nc = tc.nc
     lists_in = (offs, offs2, offs3)
     words_in = (ba_words, bb_words, bc_words)
     scales_in = (ba_scales, bb_scales, bc_scales)
     values_in = (ca, cb, cc)
     books = range(3)
+    last = E_TILES - 1
 
     with ExitStack() as ctx:
         keep = ctx.enter_context(tc.tile_pool(name="keep", bufs=1))
-        ring = ctx.enter_context(tc.tile_pool(name="ring", bufs=2))
-        shared = ctx.enter_context(tc.tile_pool(name="shared", bufs=1))
+        reuse = ctx.enter_context(tc.tile_pool(name="reuse", bufs=1))
         psum = ctx.enter_context(tc.psum_pool(name="psum", bufs=1))
-        psum2 = ctx.enter_context(tc.psum_pool(name="psum2", bufs=2))
 
         lists = [keep.tile([P, I // 16], U16, name="list%d" % k) for k in books]
-        key_words = [keep.tile([P, WINDOW + 1], I32, name="key_words%d" % k) for k in books]
-        key_scales = [keep.tile([P, WINDOW + 4], U8, name="key_scales%d" % k, tag="key_scales%d" % k, align_bytes=64)
-                      for k in books]
-        tables = [keep.tile([P, E_TILES * U + SPARE], F32, name="table%d" % k, tag="table%d" % k, align_bytes=64) for k in books]
-
-        ident = keep.tile([P, P], F32)
-        make_identity(nc, ident[:])
+        key_words = [keep.tile([P, WORD_WINDOW], I32, name="key_words%d" % k) for k in books]
+        key_bytes = [keep.tile([P, BYTE_WINDOW], U8, name="key_bytes%d" % k) for k in books]
+        tables = {(k, g): keep.tile([P, FLOAT_WINDOW], F32, name="table%d_%d" % (k, g), tag="table%d_%d" % (k, g))
+                  for k in books for g in range(E_TILES) if (k, g) != (2, 0)}
+        tables[2, 0] = reuse.tile([P, WORD_WINDOW], F32, name="last_table", offset=0, align_bytes=64)
+        planes = keep.tile([P, 3 * I], U8, align_bytes=64)
 
         first_row = P - BLOCKS
-        nc.vector.memset(key_scales[0][:first_row, :U + 4].bitcast(I32), 0)
-        nc.vector.memset(key_scales[0][:, U:].bitcast(I32), 0)
-        nc.vector.memset(key_words[0][:, U:], 0)
-        nc.vector.memset(key_scales[1][:].bitcast(I32), 0)
-        for k in (1, 2):
-            nc.vector.memset(key_words[k][:, U:], 0)
-        nc.gpsimd.memset(key_scales[2][:].bitcast(I32), 0)
-        for k in books:
-            nc.gpsimd.memset(tables[k][:, E_TILES * U:], 0.0)
-
         def load_values(k, g):
-            nc.sync.dma_start(out=tables[k][:, g * U:(g + 1) * U], in_=values_in[k][g * P:(g + 1) * P, :])
-
-        def load_scales(k):
-            for quad in range(4):
-                nc.sync.dma_start(out=key_scales[k][32 * quad:32 * quad + 4, :U].bitcast(I32),
-                                  in_=scales_in[k][0, 4 * quad:4 * quad + 4, :].bitcast(I32))
+            nc.sync.dma_start(out=tables[k, g][:, :U], in_=values_in[k][g * P:(g + 1) * P, :])
 
         def load_words(k):
             nc.sync.dma_start(out=key_words[k][:, :U],
                               in_=words_in[k][0].rearrange("p n t -> p (n t)").bitcast(I32))
 
+        def load_bytes(k):
+            nc.sync.dma_start(out=key_bytes[k][first_row:, :U].bitcast(I32), in_=scales_in[k][0].bitcast(I32))
+
         nc.sync.dma_start(lists[0][:], lists_in[0])
-        nc.sync.dma_start(out=key_scales[0][first_row:, :U].bitcast(I32), in_=scales_in[0][0].bitcast(I32))
-        load_words(0)
-        for k in (1, 2):
-            nc.sync.dma_start(lists[k][:], lists_in[k])
-            load_words(k)
+        load_bytes(0)
+        load_values(0, last)
+        nc.sync.dma_start(lists[1][:], lists_in[1])
+        load_bytes(1)
+        load_values(1, last)
+        nc.sync.dma_start(lists[2][:], lists_in[2])
+        load_values(2, last)
+        load_bytes(2)
         q_raw = keep.tile([P, PACK, Q], F32)
         nc.sync.dma_start(out=q_raw[:], in_=query.rearrange("(p j) w -> p j w", j=PACK))
-        picked_scales = [keep.tile([P, I], U8, name="picked_scales%d" % k, align_bytes=64) for k in books]
-        nc.vector.tensor_copy(out=picked_scales[0][:], in_=key_scales[0][:, :WINDOW].indirect(lists[0][:]))
-        for k in (1, 2):
-            load_scales(k)
-        last = E_TILES - 1
-        first_plane = keep.tile([P, I], U8, name="first_plane", tag="key_scales0", align_bytes=64)
-        for quad in range(4):
-            nc.sync.dma_start(out=first_plane[32 * quad:32 * quad + 4, :].bitcast(I32),
-                              in_=picked_scales[0][first_row + 4 * quad:first_row + 4 * quad + 4, :].bitcast(I32))
-        for k in books:
-            load_values(k, last)
+        load_words(0)
+        load_values(0, 2)
+        load_words(1)
+        load_words(2)
+        slot_scale = keep.tile([P, PACK], F32)
+        nc.sync.dma_start(out=slot_scale[:], in_=vsc.rearrange("(p t) o -> p (t o)", t=PACK))
+        slot_size = keep.tile([P, PACK], F32)
+        nc.sync.dma_start(out=slot_size[:], in_=size.rearrange("o (p t) -> (o p) t", t=PACK))
+        for k, g in ((1, 2), (0, 1), (1, 1), (2, 2), (2, 1), (0, 0), (1, 0), (2, 0)):
+            load_values(k, g)
 
-        q_bf = keep.tile([P, Q, PACK], BF16, align_bytes=64)
-        nc.scalar.copy(out=q_bf[:], in_=q_raw[:].rearrange("p j w -> p w j"))
-        factor_rows = q_raw[:, 0, :]
-        nc.sync.dma_start(out=factor_rows[0:PACK, :].rearrange("t (b j) -> t b j", j=RUN),
-                            in_=vsc.rearrange("(b t j) o -> t b (j o)", t=PACK, j=RUN))
-        nc.sync.dma_start(out=factor_rows[PACK:2 * PACK, :].rearrange("t (b j) -> t b j", j=RUN),
-                            in_=size.rearrange("o (b t j) -> (o t) b j", t=PACK, j=RUN))
+        warm = keep.tile([P, 1], F32)
+        nc.gpsimd.memset(warm[:], 0.0)
+        for k in books:
+            nc.vector.memset(key_bytes[k][:first_row, :U].bitcast(I32), 0)
+            nc.vector.memset(key_bytes[k][:, U:].bitcast(I32), 0)
+        for k in books:
+            nc.vector.memset(key_words[k][:, U:], 0)
+        nc.vector.memset(planes[:].bitcast(I32), 0)
+        for k in books:
+            nc.gpsimd.memset(tables[k, last][:, U:], 0.0)
+        ident = keep.tile([P, P], F32)
+        make_identity(nc, ident[:])
         for g in reversed(range(last)):
             for k in books:
-                load_values(k, g)
+                nc.gpsimd.memset(tables[k, g][:, U:], 0.0)
 
-        factors = keep.tile([P, 2 * PACK], F32)
+        picked_bytes = keep.tile([P, 3 * I], U8)
+        for k in books:
+            nc.vector.tensor_copy(out=picked_bytes[:, k * I:(k + 1) * I], in_=key_bytes[k][:].indirect(lists[k][:]))
 
+        warmed = keep.tile([P, 1], F32)
+        nc.scalar.activation(out=warmed[:], in_=warm[:], func=ACT.Exp)
+
+        def gather_on_scalar(k, g):
+            picked = keep.tile([P, I], F32, name="picked%d_%d" % (k, g))
+            nc.scalar.activation(out=picked[:], in_=tables[k, g][:].indirect(lists[k][:]), func=ACT.Copy)
+            return picked
+
+        def gather_and_add(k, g, other):
+            picked = keep.tile([P, I], F32, name="picked%d_%d" % (k, g))
+            nc.vector.tensor_tensor(out=picked[:], in0=tables[k, g][:].indirect(lists[k][:]), in1=other[:], op=ALU.add)
+            return picked
+
+        banks = [psum.tile([P, PACK, P], F32, name="value_bank%d" % g) for g in range(E_TILES)]
+
+        def turn(g, places, opens, closes):
+            for t in range(PACK):
+                nc.tensor.matmul(banks[g][:, t, :], lhsT=places[t], rhs=ident[:], is_transpose=True,
+                                 start=(opens and t == 0), stop=(closes and t == PACK - 1))
+
+        def turn_in_list_order(g, picked, opens, closes):
+            turn(g, [picked[:, t::PACK] for t in range(PACK)], opens, closes)
+
+        woven = {}
+
+        def scale_values(g):
+            if g in (1, 2):
+                woven[g] = reuse.tile([P, P, PACK], BF16, name="woven%d" % g, offset=(g - 1) * 1024, align_bytes=64)
+            else:
+                woven[g] = keep.tile([P, P, PACK], BF16, name="woven%d" % g, align_bytes=64)
+            nc.vector.tensor_tensor(
+                out=woven[g][:], in0=banks[g][:].rearrange("p t x -> p x t"),
+                in1=slot_scale[:].rearrange("p (o t) -> p o t", o=1).to_broadcast([P, P, PACK]), op=ALU.mult)
+
+        for k in books:
+            turn_in_list_order(last, gather_on_scalar(k, last), k == 0, k == 2)
+        for quad in range(4):
+            nc.scalar.dma_start(out=planes[32 * quad:32 * quad + 4, :].bitcast(I32),
+                                in_=picked_bytes[first_row + 4 * quad:first_row + 4 * quad + 4, :].bitcast(I32))
+
+        q_bf = keep.tile([P, Q, PACK], BF16, align_bytes=64)
+        nc.vector.tensor_copy(out=q_bf[:], in_=q_raw[:].rearrange("p j w -> p w j"))
         q_codes = keep.tile([P, Q], U32, align_bytes=64)
         q_scale = keep.tile([P, Q], U8, align_bytes=64)
-
-        def gather_values(g, places):
-            for k in books:
-                picked = ring.tile([P, I], F32, name="picked%d" % k)
-                window = tables[k][:, g * U:g * U + WINDOW].bitcast(U32)
-                nc.vector.tensor_copy(
-                    out=picked[:].bitcast(U32).rearrange("p (t b j) -> p b t j", t=PACK, j=RUN),
-                    in_=window.indirect(lists[k][:]))
-                for t in range(PACK):
-                    region, opens, closes = places[t]
-                    nc.tensor.matmul(region, lhsT=picked[:, t * P:(t + 1) * P], rhs=ident[:],
-                                     is_transpose=True, start=(k == 0 and opens), stop=(k == 2 and closes))
-
-        early = keep.tile([P, E_TILES, P, PACK], BF16, align_bytes=64)
-
-        def scale_on_scalar(bank, first, place):
-            scaled = ring.tile([P, PACK, P], BF16)
-            for t in range(PACK):
-                nc.scalar.activation(out=scaled[:, t, :], in_=bank[:, t * P:(t + 1) * P], func=ACT.Copy,
-                                     scale=factors[:, first + t:first + t + 1])
-            nc.scalar.copy(out=early[:, place], in_=scaled[:].rearrange("p t x -> p x t"))
+        nc.vector.quantize_mx(out=q_codes[:].bitcast(FP8X4), scales=q_scale[:],
+                              in_=q_bf[:].rearrange("p w j -> p (w j)"))
 
         picked_words = [keep.tile([P, I], U32, name="picked_words%d" % k, align_bytes=64) for k in books]
         for k in books:
-            nc.vector.tensor_copy(out=picked_words[k][:], in_=key_words[k][:, :WINDOW].bitcast(U32).indirect(lists[k][:]))
-        nc.vector.quantize_mx(out=q_codes[:].bitcast(FP8X4), scales=q_scale[:],
-                              in_=q_bf[:].rearrange("p w j -> p (w j)"))
-        for k in (1, 2):
-            nc.vector.tensor_copy(out=picked_scales[k][:], in_=key_scales[k][:, :WINDOW].indirect(lists[k][:]))
-        key_planes = (first_plane, picked_scales[1], picked_scales[2])
+            nc.vector.tensor_copy(out=picked_words[k][:], in_=key_words[k][:].bitcast(U32).indirect(lists[k][:]))
+        turn_in_list_order(2, gather_on_scalar(0, 2), True, False)
+        second2 = gather_on_scalar(1, 2)
         scores = psum.tile([P, I], F32, name="scores", tag="scores")
         for k in books:
             nc.tensor.matmul_mx(out=scores[:], lhsT=q_codes[:].bitcast(FP8X4), lhsT_scale=q_scale[:],
-                                rhs=picked_words[k][:].bitcast(FP8X4), rhs_scale=key_planes[k][:],
+                                rhs=picked_words[k][:].bitcast(FP8X4), rhs_scale=planes[:, k * I:(k + 1) * I],
                                 start=(k == 0), stop=(k == 2))
+        scale_values(last)
 
         neg_max = keep.tile([P, 1], F32)
         nc.vector.tensor_reduce(out=neg_max[:], in_=scores[:], axis=mybir.AxisListType.X, op=ALU.max, negate=True)
+        turn_in_list_order(1, gather_on_scalar(0, 1), True, False)
+        second1 = gather_on_scalar(1, 1)
         prob = keep.tile([P, I], F32)
         row_sum = keep.tile([P, 1], F32)
         nc.scalar.activation(out=prob[:], in_=scores[:], func=ACT.Exp, bias=neg_max[:], accum_out=row_sum[:])
-        inv_sum = keep.tile([P, 1], F32)
-        nc.vector.reciprocal(out=inv_sum[:], in_=row_sum[:])
-        prob_dealt = keep.tile([P, I], F32)
-        nc.scalar.activation(out=prob_dealt[:].rearrange("p (t b j) -> p t b j", t=PACK, j=RUN),
-                             in_=prob[:].rearrange("p (b t j) -> p t b j", t=PACK, j=RUN),
-                             func=ACT.Copy, scale=inv_sum[:])
-        factor_bank = psum.tile([P, P], F32, tag="narrow_bank")
-        nc.tensor.transpose(factor_bank[:], factor_rows, ident[:])
-        nc.scalar.copy(out=factors[:], in_=factor_bank[:, :2 * PACK])
-        weight_bank = psum.tile([P, PACK * P], F32, name="weight_bank", tag="weight_bank")
+        size_bank = psum.tile([P, PACK, P], F32, name="size_bank", tag="size_bank")
         for t in range(PACK):
-            nc.tensor.transpose(weight_bank[:, t * P:(t + 1) * P], prob_dealt[:, t * P:(t + 1) * P], ident[:])
-        scale_on_scalar(weight_bank, PACK, 0)
+            nc.tensor.transpose(size_bank[:, t, :], slot_size[:, t:t + 1].to_broadcast([P, P]), ident[:])
 
-        for g in reversed(range(1, E_TILES)):
-            bank = psum2.tile([P, PACK * P], F32, name="value_bank")
-            gather_values(g, [(bank[:, t * P:(t + 1) * P], t == 0, t == PACK - 1) for t in range(PACK)])
-            scale_on_scalar(bank, 0, g)
-        place0 = psum.tile([P, P], F32, name="place0", tag="scores")
-        place1 = psum.tile([P, P], F32, name="place1", tag="weight_bank")
-        pair = psum2.tile([P, 2 * P], F32, name="pair", tag="value_bank")
-        gather_values(0, [(place0[:], True, True), (place1[:], True, True),
-                          (pair[:, :P], True, False), (pair[:, P:], False, True)])
+        turn_in_list_order(2, gather_and_add(2, 2, second2), False, True)
+        turn_in_list_order(1, gather_and_add(2, 1, second1), False, True)
+        inv_sum = keep.tile([P, 1], F32, name="inv_sum", tag="table2_1")
+        nc.vector.reciprocal(out=inv_sum[:], in_=row_sum[:])
+        weights = keep.tile([P, I], BF16)
+        nc.vector.scalar_tensor_tensor(out=weights[:].rearrange("p (m t) -> p m t", t=PACK),
+                                       in0=prob[:].rearrange("p (m t) -> p m t", t=PACK), scalar=inv_sum[:],
+                                       in1=size_bank[:].rearrange("p t m -> p m t"), op0=ALU.mult, op1=ALU.mult)
+        weight_bank = psum.tile([P, 2, Q], F32, name="weight_bank")
+        for u in range(2):
+            nc.tensor.transpose(weight_bank[:, u, :], weights[:].bitcast(F32)[:, u::2], ident[:])
 
-        early_codes = keep.tile([P, E_TILES * P], U32, name="early_codes", tag="table2", align_bytes=64)
-        early_plane = keep.tile([P, E_TILES * P], U8, align_bytes=64)
-        for lo, hi in ((2, 4), (0, 1), (1, 2)):
-            nc.vector.quantize_mx(out=early_codes[:, lo * P:hi * P].bitcast(FP8X4),
-                                  scales=early_plane[:, lo * P:hi * P],
-                                  in_=early[:, lo:hi].rearrange("p g x t -> p (g x t)"))
+        turn_in_list_order(0, gather_on_scalar(0, 0), True, False)
+        turn_in_list_order(0, gather_on_scalar(1, 0), False, False)
+        weights_woven = keep.tile([P, Q * PACK], BF16, align_bytes=64)
+        nc.scalar.copy(out=weights_woven[:].bitcast(F32).rearrange("p (q u) -> p q u", u=2),
+                       in_=weight_bank[:].rearrange("p u q -> p q u"))
+        dealt = keep.tile([P, PACK, P], F32)
+        nc.vector.tensor_copy(out=dealt[:].bitcast(U32).rearrange("p t m -> p m t"),
+                              in_=tables[2, 0][:].bitcast(U32).indirect(lists[2][:]))
+        turn(0, [dealt[:, t, :] for t in range(PACK)], False, True)
 
-        def product(result_bank, codes, plane):
-            nc.tensor.matmul_mx(out=result_bank, lhsT=early_codes[:, :P].bitcast(FP8X4), lhsT_scale=early_plane[:, :P],
-                                rhs=codes.bitcast(FP8X4), rhs_scale=plane, start=True, stop=True)
+        w_codes = keep.tile([P, Q], U32, align_bytes=64)
+        w_scale = keep.tile([P, Q], U8, align_bytes=64)
+        v_codes = keep.tile([P, E], U32, align_bytes=64)
+        v_scale = keep.tile([P, E], U8, align_bytes=64)
 
-        half = P // 2
-        halves = range(2)
-        woven = [shared.tile([P, half, PACK], BF16, name="woven%d" % h, align_bytes=64) for h in halves]
-        for h in halves:
-            for t, place in enumerate((place0, place1)):
-                nc.scalar.activation(out=woven[h][:, :, t], in_=place[:, h * half:(h + 1) * half], func=ACT.Copy,
-                                     scale=factors[:, t:t + 1])
+        def quantise(g):
+            cols = slice(g * P, (g + 1) * P)
+            nc.vector.quantize_mx(out=v_codes[:, cols].bitcast(FP8X4), scales=v_scale[:, cols],
+                                  in_=woven[g][:].rearrange("p x t -> p (x t)"))
 
-        for lo, hi, tag in ((2 * P, E, "wide_bank"), (P, 2 * P, "narrow_bank")):
-            early_bank = psum.tile([P, hi - lo], F32, name="early_" + tag, tag=tag)
-            product(early_bank[:], early_codes[:, lo:hi], early_plane[:, lo:hi])
-            early_result = (keep if hi - lo > P else shared).tile([P, hi - lo], F32, name="result_" + tag)
-            nc.scalar.copy(out=early_result[:], in_=early_bank[:])
-            nc.sync.dma_start(out=out[:, lo:hi], in_=early_result[:])
+        def finish(lo, hi, tag, copy):
+            cols = slice(lo * P, hi * P)
+            result_bank = psum.tile([P, (hi - lo) * P], F32, name="result_" + tag, tag=tag)
+            nc.tensor.matmul_mx(out=result_bank[:], lhsT=w_codes[:].bitcast(FP8X4), lhsT_scale=w_scale[:],
+                                rhs=v_codes[:, cols].bitcast(FP8X4), rhs_scale=v_scale[:, cols],
+                                start=True, stop=True)
+            result = keep.tile([P, (hi - lo) * P], F32, name="result%d" % lo)
+            copy(out=result[:], in_=result_bank[:])
+            nc.sync.dma_start(out=out[:, cols], in_=result[:])
 
-        late_codes = [keep.tile([P, half], U32, name="late_codes%d" % h, align_bytes=64) for h in halves]
-        late_plane = [keep.tile([P, half], U8, name="late_plane%d" % h, align_bytes=64) for h in halves]
-        late_bank = [psum.tile([P, half], F32, name="late_bank%d" % h) for h in halves]
-        late_result = keep.tile([P, P], F32)
-        for h in halves:
-            nc.vector.tensor_tensor(
-                out=woven[h][:, :, 2:], in0=pair[:].rearrange("p (t e) -> p e t", t=2)[:, h * half:(h + 1) * half, :],
-                in1=factors[:, 2:PACK].rearrange("p (o t) -> p o t", o=1).to_broadcast([P, half, 2]),
-                op=ALU.mult)
-        for h in halves:
-            nc.vector.quantize_mx(out=late_codes[h][:].bitcast(FP8X4), scales=late_plane[h][:],
-                                  in_=woven[h][:].rearrange("p x t -> p (x t)"))
-            product(late_bank[h][:], late_codes[h][:], late_plane[h][:])
-        nc.scalar.copy(out=late_result[:, :half], in_=late_bank[0][:])
-        nc.vector.tensor_copy(out=late_result[:, half:], in_=late_bank[1][:])
-        nc.sync.dma_start(out=out[:, :P], in_=late_result[:])
+        quantise(3)
+        scale_values(2)
+        nc.vector.quantize_mx(out=w_codes[:].bitcast(FP8X4), scales=w_scale[:], in_=weights_woven[:])
+        quantise(2)
+        finish(2, 4, "scores", nc.scalar.copy)
+        scale_values(1)
+        quantise(1)
+        finish(1, 2, "size_bank", nc.scalar.copy)
+        scale_values(0)
+        quantise(0)
+        finish(0, 1, "last_bank", nc.scalar.copy)

@@ -132,8 +132,10 @@ def tile_attend_additivekeys_kernel(tc, query, ba_words, ba_scales, bb_words, bb
             else:
                 woven[g] = keep.tile([P, P, PACK], BF16, name="woven%d" % g, align_bytes=64)
             nc.vector.tensor_tensor(
-                out=woven[g][:], in0=banks[g][:].rearrange("p t x -> p x t"),
-                in1=slot_scale[:].rearrange("p (o t) -> p o t", o=1).to_broadcast([P, P, PACK]), op=ALU.mult)
+                out=woven[g][:].rearrange("p (c i) t -> p c t i", i=PACK),
+                in0=banks[g][:].rearrange("p t (c i) -> p c t i", i=PACK),
+                in1=slot_scale[:].rearrange("p (c t i) -> p c t i", c=1, i=1).to_broadcast([P, P // PACK, PACK, PACK]),
+                op=ALU.mult)
 
         for k in books:
             turn_in_list_order(last, gather_on_scalar(k, last), k == 0, k == 2)

@@ -33,23 +33,27 @@ def tile_attend_additivekeys_kernel(tc, query, ba_words, ba_scales, bb_words, bb
     scales_in = (ba_scales, bb_scales, bc_scales)
     values_in = (ca, cb, cc)
     books = range(3)
-    last = E_TILES - 1
 
     with ExitStack() as ctx:
         keep = ctx.enter_context(tc.tile_pool(name="keep", bufs=1))
-        reuse = ctx.enter_context(tc.tile_pool(name="reuse", bufs=1))
         psum = ctx.enter_context(tc.psum_pool(name="psum", bufs=1))
 
-        lists = [keep.tile([P, I // 16], U16, name="list%d" % k) for k in books]
-        key_words = [keep.tile([P, WORD_WINDOW], I32, name="key_words%d" % k) for k in books]
-        key_bytes = [keep.tile([P, BYTE_WINDOW], U8, name="key_bytes%d" % k) for k in books]
-        tables = {(k, g): keep.tile([P, FLOAT_WINDOW], F32, name="table%d_%d" % (k, g), tag="table%d_%d" % (k, g))
-                  for k in books for g in range(E_TILES) if (k, g) != (2, 0)}
-        tables[2, 0] = reuse.tile([P, WORD_WINDOW], F32, name="last_table", offset=0, align_bytes=64)
-        planes = keep.tile([P, 3 * I], U8, align_bytes=64)
+        def sbuf(shape, dtype, name, over=None):
+            return keep.tile(shape, dtype, name=name, tag=over or name, align_bytes=64)
 
+        lists = [keep.tile([P, I // 16], U16, name="list%d" % k) for k in books]
+        key_words = [sbuf([P, WORD_WINDOW], I32, "key_words%d" % k) for k in books]
+        key_bytes = [sbuf([P, BYTE_WINDOW], U8, "key_bytes%d" % k) for k in books]
         first_row = P - BLOCKS
-        def load_values(k, g):
+        tables = {}
+        rooms = {}
+
+        def load_list(k):
+            nc.sync.dma_start(lists[k][:], lists_in[k])
+
+        def load_values(k, g, over=None, width=FLOAT_WINDOW):
+            rooms[k, g] = over or "table%d_%d" % (k, g)
+            tables[k, g] = sbuf([P, width], F32, "table%d_%d" % (k, g), rooms[k, g])
             nc.sync.dma_start(out=tables[k, g][:, :U], in_=values_in[k][g * P:(g + 1) * P, :])
 
         def load_words(k):
@@ -59,62 +63,41 @@ def tile_attend_additivekeys_kernel(tc, query, ba_words, ba_scales, bb_words, bb
         def load_bytes(k):
             nc.sync.dma_start(out=key_bytes[k][first_row:, :U].bitcast(I32), in_=scales_in[k][0].bitcast(I32))
 
-        nc.sync.dma_start(lists[0][:], lists_in[0])
-        load_bytes(0)
-        load_values(0, last)
-        nc.sync.dma_start(lists[1][:], lists_in[1])
-        load_bytes(1)
-        load_values(1, last)
-        nc.sync.dma_start(lists[2][:], lists_in[2])
-        load_values(2, last)
+        for k in books:
+            load_list(k)
+            if k < 2:
+                load_bytes(k)
+            load_values(k, 3)
         load_bytes(2)
-        q_raw = keep.tile([P, PACK, Q], F32)
-        nc.sync.dma_start(out=q_raw[:], in_=query.rearrange("(p j) w -> p j w", j=PACK))
         load_words(0)
         load_values(0, 2)
-        load_words(1)
-        load_words(2)
-        slot_scale = keep.tile([P, PACK], F32)
-        nc.sync.dma_start(out=slot_scale[:], in_=vsc.rearrange("(p t) o -> p (t o)", t=PACK))
-        slot_size = keep.tile([P, PACK], F32)
+        slot_size = sbuf([P, PACK], F32, "slot_size")
         nc.sync.dma_start(out=slot_size[:], in_=size.rearrange("o (p t) -> (o p) t", t=PACK))
-        for k, g in ((1, 2), (0, 1), (1, 1), (2, 2), (2, 1), (0, 0), (1, 0), (2, 0)):
-            load_values(k, g)
+        q_raw = sbuf([P, PACK, Q], F32, "q_raw")
+        nc.sync.dma_start(out=q_raw[:], in_=query.rearrange("(p j) w -> p j w", j=PACK))
+        load_words(1)
+        load_values(1, 2)
+        load_words(2)
+        load_values(1, 1)
+        slot_scale = sbuf([P, PACK], F32, "slot_scale")
+        nc.sync.dma_start(out=slot_scale[:], in_=vsc.rearrange("(p t) o -> p (t o)", t=PACK))
+
+        for k in books:
+            nc.vector.memset(key_bytes[k][:first_row, :U + 4].bitcast(I32), 0)
 
         warm = keep.tile([P, 1], F32)
         nc.gpsimd.memset(warm[:], 0.0)
-        for k in books:
-            nc.vector.memset(key_bytes[k][:first_row, :U].bitcast(I32), 0)
-            nc.vector.memset(key_bytes[k][:, U:].bitcast(I32), 0)
-        for k in books:
-            nc.vector.memset(key_words[k][:, U:], 0)
-        nc.vector.memset(planes[:].bitcast(I32), 0)
-        for k in books:
-            nc.gpsimd.memset(tables[k, last][:, U:], 0.0)
-        ident = keep.tile([P, P], F32)
-        make_identity(nc, ident[:])
-        for g in reversed(range(last)):
-            for k in books:
-                nc.gpsimd.memset(tables[k, g][:, U:], 0.0)
-
-        picked_bytes = keep.tile([P, 3 * I], U8)
-        for k in books:
-            nc.vector.tensor_copy(out=picked_bytes[:, k * I:(k + 1) * I], in_=key_bytes[k][:].indirect(lists[k][:]))
-
         warmed = keep.tile([P, 1], F32)
         nc.scalar.activation(out=warmed[:], in_=warm[:], func=ACT.Exp)
+        ident = keep.tile([P, P], F32)
+        make_identity(nc, ident[:])
 
-        def gather_on_scalar(k, g):
-            picked = keep.tile([P, I], F32, name="picked%d_%d" % (k, g))
+        banks = {g: psum.tile([P, PACK, P], F32, name="value_bank%d" % g, tag="value_bank%d" % g) for g in (3, 2, 0)}
+
+        def gather_on_scalar(k, g, over=None):
+            picked = sbuf([P, I], F32, "picked%d_%d" % (k, g), over)
             nc.scalar.activation(out=picked[:], in_=tables[k, g][:].indirect(lists[k][:]), func=ACT.Copy)
             return picked
-
-        def gather_and_add(k, g, other):
-            picked = keep.tile([P, I], F32, name="picked%d_%d" % (k, g))
-            nc.vector.tensor_tensor(out=picked[:], in0=tables[k, g][:].indirect(lists[k][:]), in1=other[:], op=ALU.add)
-            return picked
-
-        banks = [psum.tile([P, PACK, P], F32, name="value_bank%d" % g) for g in range(E_TILES)]
 
         def turn(g, places, opens, closes):
             for t in range(PACK):
@@ -124,105 +107,120 @@ def tile_attend_additivekeys_kernel(tc, query, ba_words, ba_scales, bb_words, bb
         def turn_in_list_order(g, picked, opens, closes):
             turn(g, [picked[:, t::PACK] for t in range(PACK)], opens, closes)
 
-        woven = {}
+        def gather_and_add(g, second):
+            both = sbuf([P, I], F32, "both%d" % g)
+            nc.vector.tensor_tensor(out=both[:], in0=tables[2, g][:].indirect(lists[2][:]), in1=second[:], op=ALU.add)
+            return both
 
-        def scale_values(g):
-            if g in (1, 2):
-                woven[g] = reuse.tile([P, P, PACK], BF16, name="woven%d" % g, offset=(g - 1) * 1024, align_bytes=64)
-            else:
-                woven[g] = keep.tile([P, P, PACK], BF16, name="woven%d" % g, align_bytes=64)
+        def scale_values(g, woven):
             nc.vector.tensor_tensor(
-                out=woven[g][:].rearrange("p (c i) t -> p c t i", i=PACK),
+                out=woven.rearrange("p (c i) t -> p c t i", i=PACK),
                 in0=banks[g][:].rearrange("p t (c i) -> p c t i", i=PACK),
                 in1=slot_scale[:].rearrange("p (c t i) -> p c t i", c=1, i=1).to_broadcast([P, P // PACK, PACK, PACK]),
                 op=ALU.mult)
 
+        picked_bytes = keep.tile([P, 3 * I], U8)
         for k in books:
-            turn_in_list_order(last, gather_on_scalar(k, last), k == 0, k == 2)
+            nc.vector.tensor_copy(out=picked_bytes[:, k * I:(k + 1) * I], in_=key_bytes[k][:].indirect(lists[k][:]))
+        turn_in_list_order(3, gather_on_scalar(0, 3), True, False)
+        planes = sbuf([P, 3 * I], U8, "planes", rooms[0, 3])
         for quad in range(4):
-            nc.scalar.dma_start(out=planes[32 * quad:32 * quad + 4, :].bitcast(I32),
-                                in_=picked_bytes[first_row + 4 * quad:first_row + 4 * quad + 4, :].bitcast(I32))
+            nc.sync.dma_start(out=planes[32 * quad:32 * quad + 4, :].bitcast(I32),
+                              in_=picked_bytes[first_row + 4 * quad:first_row + 4 * quad + 4, :].bitcast(I32))
+        load_values(2, 2, "key_bytes2")
+        turn_in_list_order(3, gather_on_scalar(1, 3), False, False)
+        size_bank = psum.tile([P, P, PACK], F32, name="size_bank", tag="size_bank")
+        for t in range(PACK):
+            nc.tensor.transpose(size_bank[:, :, t], slot_size[:, t:t + 1].to_broadcast([P, P]), ident[:])
+        turn_in_list_order(3, gather_on_scalar(2, 3), False, True)
+        load_values(0, 1, rooms[2, 3])
 
-        q_bf = keep.tile([P, Q, PACK], BF16, align_bytes=64)
-        nc.vector.tensor_copy(out=q_bf[:], in_=q_raw[:].rearrange("p j w -> p w j"))
-        q_codes = keep.tile([P, Q], U32, align_bytes=64)
-        q_scale = keep.tile([P, Q], U8, align_bytes=64)
+        picked_words = [sbuf([P, I], U32, "picked_words%d" % k) for k in books]
+
+        def gather_words(k):
+            nc.vector.tensor_copy(out=picked_words[k][:], in_=key_words[k][:].bitcast(U32).indirect(lists[k][:]))
+
+        gather_words(0)
+        load_values(2, 1, "key_words0")
+        turn_in_list_order(2, gather_on_scalar(0, 2), True, False)
+        load_values(0, 0, rooms[0, 2])
+        q_bf = sbuf([P, Q, PACK], BF16, "q_bf")
+        nc.gpsimd.tensor_copy(out=q_bf[:], in_=q_raw[:].rearrange("p j w -> p w j"))
+        gather_words(1)
+        q_codes = sbuf([P, Q], U32, "q_codes", "key_words1")
+        q_scale = sbuf([P, Q], U8, "q_scale")
         nc.vector.quantize_mx(out=q_codes[:].bitcast(FP8X4), scales=q_scale[:],
                               in_=q_bf[:].rearrange("p w j -> p (w j)"))
-
-        picked_words = [keep.tile([P, I], U32, name="picked_words%d" % k, align_bytes=64) for k in books]
-        for k in books:
-            nc.vector.tensor_copy(out=picked_words[k][:], in_=key_words[k][:].bitcast(U32).indirect(lists[k][:]))
-        turn_in_list_order(2, gather_on_scalar(0, 2), True, False)
         second2 = gather_on_scalar(1, 2)
+        load_values(1, 0, rooms[1, 2])
+        gather_words(2)
+        load_values(2, 0, "key_words2", WORD_WINDOW)
+
         scores = psum.tile([P, I], F32, name="scores", tag="scores")
         for k in books:
             nc.tensor.matmul_mx(out=scores[:], lhsT=q_codes[:].bitcast(FP8X4), lhsT_scale=q_scale[:],
                                 rhs=picked_words[k][:].bitcast(FP8X4), rhs_scale=planes[:, k * I:(k + 1) * I],
                                 start=(k == 0), stop=(k == 2))
-        scale_values(last)
 
-        neg_max = keep.tile([P, 1], F32)
+        both2 = gather_and_add(2, second2)
+        neg_max = sbuf([P, 1], F32, "neg_max", rooms[2, 2])
         nc.vector.tensor_reduce(out=neg_max[:], in_=scores[:], axis=mybir.AxisListType.X, op=ALU.max, negate=True)
-        turn_in_list_order(1, gather_on_scalar(0, 1), True, False)
+        woven3 = sbuf([P, P, PACK], BF16, "woven3", "picked1_2")
+        scale_values(3, woven3[:])
+        banks[1] = psum.tile([P, PACK, P], F32, name="value_bank1", tag="value_bank3")
         second1 = gather_on_scalar(1, 1)
-        prob = keep.tile([P, I], F32)
+        turn_in_list_order(1, gather_on_scalar(0, 1), True, False)
+        prob = sbuf([P, I], F32, "prob", rooms[0, 1])
         row_sum = keep.tile([P, 1], F32)
         nc.scalar.activation(out=prob[:], in_=scores[:], func=ACT.Exp, bias=neg_max[:], accum_out=row_sum[:])
-        size_bank = psum.tile([P, PACK, P], F32, name="size_bank", tag="size_bank")
-        for t in range(PACK):
-            nc.tensor.transpose(size_bank[:, t, :], slot_size[:, t:t + 1].to_broadcast([P, P]), ident[:])
+        turn_in_list_order(2, both2, False, True)
+        turn_in_list_order(1, gather_and_add(1, second1), False, True)
 
-        turn_in_list_order(2, gather_and_add(2, 2, second2), False, True)
-        turn_in_list_order(1, gather_and_add(2, 1, second1), False, True)
-        inv_sum = keep.tile([P, 1], F32, name="inv_sum", tag="table2_1")
+        inv_sum = sbuf([P, 1], F32, "inv_sum", rooms[2, 1])
         nc.vector.reciprocal(out=inv_sum[:], in_=row_sum[:])
+        codes = sbuf([P, 5 * P], U32, "codes", "picked1_1")
+        plane = sbuf([P, 5 * P], U8, "plane")
+
+        def quantise(place, count, woven):
+            cols = slice(place * P, (place + count) * P)
+            nc.vector.quantize_mx(out=codes[:, cols].bitcast(FP8X4), scales=plane[:, cols], in_=woven)
+
+        quantise(2, 1, woven3[:].rearrange("p x t -> p (x t)"))
         weights = keep.tile([P, I], BF16)
-        nc.vector.scalar_tensor_tensor(out=weights[:].rearrange("p (m t) -> p m t", t=PACK),
-                                       in0=prob[:].rearrange("p (m t) -> p m t", t=PACK), scalar=inv_sum[:],
-                                       in1=size_bank[:].rearrange("p t m -> p m t"), op0=ALU.mult, op1=ALU.mult)
+        nc.vector.scalar_tensor_tensor(out=weights[:], in0=prob[:], scalar=inv_sum[:],
+                                       in1=size_bank[:].rearrange("p m t -> p (m t)"), op0=ALU.mult, op1=ALU.mult)
         weight_bank = psum.tile([P, 2, Q], F32, name="weight_bank")
         for u in range(2):
             nc.tensor.transpose(weight_bank[:, u, :], weights[:].bitcast(F32)[:, u::2], ident[:])
 
-        turn_in_list_order(0, gather_on_scalar(0, 0), True, False)
+        turn_in_list_order(0, gather_on_scalar(0, 0, rooms[2, 2]), True, False)
         turn_in_list_order(0, gather_on_scalar(1, 0), False, False)
-        weights_woven = keep.tile([P, Q * PACK], BF16, align_bytes=64)
-        nc.scalar.copy(out=weights_woven[:].bitcast(F32).rearrange("p (q u) -> p q u", u=2),
-                       in_=weight_bank[:].rearrange("p u q -> p q u"))
-        dealt = keep.tile([P, PACK, P], F32)
+        dealt = sbuf([P, PACK, P], F32, "dealt")
         nc.vector.tensor_copy(out=dealt[:].bitcast(U32).rearrange("p t m -> p m t"),
                               in_=tables[2, 0][:].bitcast(U32).indirect(lists[2][:]))
         turn(0, [dealt[:, t, :] for t in range(PACK)], False, True)
 
-        w_codes = keep.tile([P, Q], U32, align_bytes=64)
-        w_scale = keep.tile([P, Q], U8, align_bytes=64)
-        v_codes = keep.tile([P, E], U32, align_bytes=64)
-        v_scale = keep.tile([P, E], U8, align_bytes=64)
+        middle = sbuf([P, 3, P, PACK], BF16, "middle", rooms[2, 0])
+        nc.scalar.copy(out=middle[:, 0].rearrange("p q t -> p (q t)").bitcast(F32).rearrange("p (q u) -> p q u", u=2),
+                       in_=weight_bank[:].rearrange("p u q -> p q u"))
 
-        def quantise(g):
-            cols = slice(g * P, (g + 1) * P)
-            nc.vector.quantize_mx(out=v_codes[:, cols].bitcast(FP8X4), scales=v_scale[:, cols],
-                                  in_=woven[g][:].rearrange("p x t -> p (x t)"))
-
-        def finish(lo, hi, tag, copy):
-            cols = slice(lo * P, hi * P)
+        def finish(place, lo, hi, tag):
+            cols = slice(place * P, (place + hi - lo) * P)
             result_bank = psum.tile([P, (hi - lo) * P], F32, name="result_" + tag, tag=tag)
-            nc.tensor.matmul_mx(out=result_bank[:], lhsT=w_codes[:].bitcast(FP8X4), lhsT_scale=w_scale[:],
-                                rhs=v_codes[:, cols].bitcast(FP8X4), rhs_scale=v_scale[:, cols],
+            nc.tensor.matmul_mx(out=result_bank[:], lhsT=codes[:, :P].bitcast(FP8X4), lhsT_scale=plane[:, :P],
+                                rhs=codes[:, cols].bitcast(FP8X4), rhs_scale=plane[:, cols],
                                 start=True, stop=True)
             result = keep.tile([P, (hi - lo) * P], F32, name="result%d" % lo)
-            copy(out=result[:], in_=result_bank[:])
-            nc.sync.dma_start(out=out[:, cols], in_=result[:])
+            nc.scalar.copy(out=result[:], in_=result_bank[:])
+            nc.sync.dma_start(out=out[:, lo * P:hi * P], in_=result[:])
 
-        quantise(3)
-        scale_values(2)
-        nc.vector.quantize_mx(out=w_codes[:].bitcast(FP8X4), scales=w_scale[:], in_=weights_woven[:])
-        quantise(2)
-        finish(2, 4, "scores", nc.scalar.copy)
-        scale_values(1)
-        quantise(1)
-        finish(1, 2, "size_bank", nc.scalar.copy)
-        scale_values(0)
-        quantise(0)
-        finish(0, 1, "last_bank", nc.scalar.copy)
+        scale_values(2, middle[:, 1])
+        scale_values(1, middle[:, 2])
+        quantise(0, 2, middle[:, :2].rearrange("p g x t -> p (g x t)"))
+        finish(1, 2, 4, "scores")
+        quantise(3, 1, middle[:, 2].rearrange("p x t -> p (x t)"))
+        finish(3, 1, 2, "size_bank")
+        woven0 = sbuf([P, P, PACK], BF16, "woven0")
+        scale_values(0, woven0[:])
+        quantise(4, 1, woven0[:].rearrange("p x t -> p (x t)"))
+        finish(4, 0, 1, "last_bank")

@@ -69,16 +69,15 @@ def tile_attend_additivekeys_kernel(tc, query, ba_words, ba_scales, bb_words, bb
                 load_bytes(k)
             load_values(k, 3)
         load_bytes(2)
-        load_words(0)
-        load_values(0, 2)
-        slot_size = sbuf([P, PACK], F32, "slot_size")
-        nc.sync.dma_start(out=slot_size[:], in_=size.rearrange("o (p t) -> (o p) t", t=PACK))
         q_raw = sbuf([P, PACK, Q], F32, "q_raw")
         nc.sync.dma_start(out=q_raw[:], in_=query.rearrange("(p j) w -> p j w", j=PACK))
-        load_words(1)
+        load_words(0)
         load_values(1, 2)
-        load_words(2)
+        slot_size = sbuf([P, PACK], F32, "slot_size")
+        nc.sync.dma_start(out=slot_size[:], in_=size.rearrange("o (p t) -> (o p) t", t=PACK))
+        load_words(1)
         load_values(1, 1)
+        load_words(2)
         slot_scale = sbuf([P, PACK], F32, "slot_scale")
         nc.sync.dma_start(out=slot_scale[:], in_=vsc.rearrange("(p t) o -> p (t o)", t=PACK))
 
@@ -92,7 +91,7 @@ def tile_attend_additivekeys_kernel(tc, query, ba_words, ba_scales, bb_words, bb
         ident = keep.tile([P, P], F32)
         make_identity(nc, ident[:])
 
-        banks = {g: psum.tile([P, PACK, P], F32, name="value_bank%d" % g, tag="value_bank%d" % g) for g in (3, 2, 0)}
+        banks = [psum.tile([P, PACK, P], F32, name="value_bank%d" % g) for g in range(E_TILES)]
 
         def gather_on_scalar(k, g, over=None):
             picked = sbuf([P, I], F32, "picked%d_%d" % (k, g), over)
@@ -133,7 +132,7 @@ def tile_attend_additivekeys_kernel(tc, query, ba_words, ba_scales, bb_words, bb
         for t in range(PACK):
             nc.tensor.transpose(size_bank[:, :, t], slot_size[:, t:t + 1].to_broadcast([P, P]), ident[:])
         turn_in_list_order(3, gather_on_scalar(2, 3), False, True)
-        load_values(0, 1, rooms[2, 3])
+        load_values(0, 2, rooms[2, 3])
 
         picked_words = [sbuf([P, I], U32, "picked_words%d" % k) for k in books]
 
@@ -141,20 +140,23 @@ def tile_attend_additivekeys_kernel(tc, query, ba_words, ba_scales, bb_words, bb
             nc.vector.tensor_copy(out=picked_words[k][:], in_=key_words[k][:].bitcast(U32).indirect(lists[k][:]))
 
         gather_words(0)
-        load_values(2, 1, "key_words0")
-        turn_in_list_order(2, gather_on_scalar(0, 2), True, False)
-        load_values(0, 0, rooms[0, 2])
+        load_values(0, 1, "key_words0")
+        second2 = gather_on_scalar(1, 2)
+        load_values(2, 1, rooms[1, 2])
         q_bf = sbuf([P, Q, PACK], BF16, "q_bf")
         nc.gpsimd.tensor_copy(out=q_bf[:], in_=q_raw[:].rearrange("p j w -> p w j"))
         gather_words(1)
-        q_codes = sbuf([P, Q], U32, "q_codes", "key_words1")
+        load_values(0, 0, "key_words1")
+        q_codes = sbuf([P, Q], U32, "q_codes")
         q_scale = sbuf([P, Q], U8, "q_scale")
         nc.vector.quantize_mx(out=q_codes[:].bitcast(FP8X4), scales=q_scale[:],
                               in_=q_bf[:].rearrange("p w j -> p (w j)"))
-        second2 = gather_on_scalar(1, 2)
-        load_values(1, 0, rooms[1, 2])
+        second1 = gather_on_scalar(1, 1)
+        load_values(2, 0, rooms[1, 1], WORD_WINDOW)
         gather_words(2)
-        load_values(2, 0, "key_words2", WORD_WINDOW)
+        load_values(1, 0, "key_words2")
+        woven3 = sbuf([P, P, PACK], BF16, "woven3")
+        scale_values(3, woven3[:])
 
         scores = psum.tile([P, I], F32, name="scores", tag="scores")
         for k in books:
@@ -162,21 +164,18 @@ def tile_attend_additivekeys_kernel(tc, query, ba_words, ba_scales, bb_words, bb
                                 rhs=picked_words[k][:].bitcast(FP8X4), rhs_scale=planes[:, k * I:(k + 1) * I],
                                 start=(k == 0), stop=(k == 2))
 
+        turn_in_list_order(2, gather_on_scalar(0, 2), True, False)
         both2 = gather_and_add(2, second2)
-        neg_max = sbuf([P, 1], F32, "neg_max", rooms[2, 2])
+        neg_max = sbuf([P, 1], F32, "neg_max")
         nc.vector.tensor_reduce(out=neg_max[:], in_=scores[:], axis=mybir.AxisListType.X, op=ALU.max, negate=True)
-        woven3 = sbuf([P, P, PACK], BF16, "woven3", "picked1_2")
-        scale_values(3, woven3[:])
-        banks[1] = psum.tile([P, PACK, P], F32, name="value_bank1", tag="value_bank3")
-        second1 = gather_on_scalar(1, 1)
+        turn_in_list_order(2, both2, False, True)
         turn_in_list_order(1, gather_on_scalar(0, 1), True, False)
-        prob = sbuf([P, I], F32, "prob", rooms[0, 1])
+        prob = sbuf([P, I], F32, "prob")
         row_sum = keep.tile([P, 1], F32)
         nc.scalar.activation(out=prob[:], in_=scores[:], func=ACT.Exp, bias=neg_max[:], accum_out=row_sum[:])
-        turn_in_list_order(2, both2, False, True)
         turn_in_list_order(1, gather_and_add(1, second1), False, True)
 
-        inv_sum = sbuf([P, 1], F32, "inv_sum", rooms[2, 1])
+        inv_sum = sbuf([P, 1], F32, "inv_sum")
         nc.vector.reciprocal(out=inv_sum[:], in_=row_sum[:])
         codes = sbuf([P, 5 * P], U32, "codes", "picked1_1")
         plane = sbuf([P, 5 * P], U8, "plane")
@@ -193,14 +192,15 @@ def tile_attend_additivekeys_kernel(tc, query, ba_words, ba_scales, bb_words, bb
         for u in range(2):
             nc.tensor.transpose(weight_bank[:, u, :], weights[:].bitcast(F32)[:, u::2], ident[:])
 
-        turn_in_list_order(0, gather_on_scalar(0, 0, rooms[2, 2]), True, False)
-        turn_in_list_order(0, gather_on_scalar(1, 0), False, False)
+        turn_in_list_order(0, gather_on_scalar(0, 0), True, False)
+        second0 = gather_on_scalar(1, 0)
         dealt = sbuf([P, PACK, P], F32, "dealt")
         nc.vector.tensor_copy(out=dealt[:].bitcast(U32).rearrange("p t m -> p m t"),
                               in_=tables[2, 0][:].bitcast(U32).indirect(lists[2][:]))
-        turn(0, [dealt[:, t, :] for t in range(PACK)], False, True)
+        turn(0, [dealt[:, t, :] for t in range(PACK)], False, False)
+        turn_in_list_order(0, second0, False, True)
 
-        middle = sbuf([P, 3, P, PACK], BF16, "middle", rooms[2, 0])
+        middle = sbuf([P, 3, P, PACK], BF16, "middle", "prob")
         nc.scalar.copy(out=middle[:, 0].rearrange("p q t -> p (q t)").bitcast(F32).rearrange("p (q u) -> p q u", u=2),
                        in_=weight_bank[:].rearrange("p u q -> p q u"))
 

@@ -72,11 +72,11 @@ def tile_attend_additivekeys_kernel(tc, query, ba_words, ba_scales, bb_words, bb
         q_raw = sbuf([P, PACK, Q], F32, "q_raw")
         nc.sync.dma_start(out=q_raw[:], in_=query.rearrange("(p j) w -> p j w", j=PACK))
         load_words(0)
-        load_values(1, 2)
+        load_values(0, 2)
         slot_size = sbuf([P, PACK], F32, "slot_size")
         nc.sync.dma_start(out=slot_size[:], in_=size.rearrange("o (p t) -> (o p) t", t=PACK))
         load_words(1)
-        load_values(1, 1)
+        load_values(1, 2)
         load_words(2)
         slot_scale = sbuf([P, PACK], F32, "slot_scale")
         nc.sync.dma_start(out=slot_scale[:], in_=vsc.rearrange("(p t) o -> p (t o)", t=PACK))
@@ -111,11 +111,12 @@ def tile_attend_additivekeys_kernel(tc, query, ba_words, ba_scales, bb_words, bb
             nc.vector.tensor_tensor(out=both[:], in0=tables[2, g][:].indirect(lists[2][:]), in1=second[:], op=ALU.add)
             return both
 
-        def scale_values(g, woven):
+        def scale_values(g, woven, lo=0, hi=P):
             nc.vector.tensor_tensor(
                 out=woven.rearrange("p (c i) t -> p c t i", i=PACK),
-                in0=banks[g][:].rearrange("p t (c i) -> p c t i", i=PACK),
-                in1=slot_scale[:].rearrange("p (c t i) -> p c t i", c=1, i=1).to_broadcast([P, P // PACK, PACK, PACK]),
+                in0=banks[g][:, :, lo:hi].rearrange("p t (c i) -> p c t i", i=PACK),
+                in1=slot_scale[:].rearrange("p (c t i) -> p c t i", c=1, i=1).to_broadcast(
+                    [P, (hi - lo) // PACK, PACK, PACK]),
                 op=ALU.mult)
 
         picked_bytes = keep.tile([P, 3 * I], U8)
@@ -132,7 +133,7 @@ def tile_attend_additivekeys_kernel(tc, query, ba_words, ba_scales, bb_words, bb
         for t in range(PACK):
             nc.tensor.transpose(size_bank[:, :, t], slot_size[:, t:t + 1].to_broadcast([P, P]), ident[:])
         turn_in_list_order(3, gather_on_scalar(2, 3), False, True)
-        load_values(0, 2, rooms[2, 3])
+        load_values(1, 1, rooms[2, 3])
 
         picked_words = [sbuf([P, I], U32, "picked_words%d" % k) for k in books]
 
@@ -141,8 +142,8 @@ def tile_attend_additivekeys_kernel(tc, query, ba_words, ba_scales, bb_words, bb
 
         gather_words(0)
         load_values(0, 1, "key_words0")
-        second2 = gather_on_scalar(1, 2)
-        load_values(2, 1, rooms[1, 2])
+        turn_in_list_order(2, gather_on_scalar(0, 2), True, False)
+        load_values(2, 1, rooms[0, 2])
         q_bf = sbuf([P, Q, PACK], BF16, "q_bf")
         nc.gpsimd.tensor_copy(out=q_bf[:], in_=q_raw[:].rearrange("p j w -> p w j"))
         gather_words(1)
@@ -151,8 +152,8 @@ def tile_attend_additivekeys_kernel(tc, query, ba_words, ba_scales, bb_words, bb
         q_scale = sbuf([P, Q], U8, "q_scale")
         nc.vector.quantize_mx(out=q_codes[:].bitcast(FP8X4), scales=q_scale[:],
                               in_=q_bf[:].rearrange("p w j -> p (w j)"))
-        second1 = gather_on_scalar(1, 1)
-        load_values(2, 0, rooms[1, 1], WORD_WINDOW)
+        second2 = gather_on_scalar(1, 2)
+        load_values(2, 0, rooms[1, 2], WORD_WINDOW)
         gather_words(2)
         load_values(1, 0, "key_words2")
         woven3 = sbuf([P, P, PACK], BF16, "woven3")
@@ -164,7 +165,7 @@ def tile_attend_additivekeys_kernel(tc, query, ba_words, ba_scales, bb_words, bb
                                 rhs=picked_words[k][:].bitcast(FP8X4), rhs_scale=planes[:, k * I:(k + 1) * I],
                                 start=(k == 0), stop=(k == 2))
 
-        turn_in_list_order(2, gather_on_scalar(0, 2), True, False)
+        second1 = gather_on_scalar(1, 1)
         both2 = gather_and_add(2, second2)
         neg_max = sbuf([P, 1], F32, "neg_max")
         nc.vector.tensor_reduce(out=neg_max[:], in_=scores[:], axis=mybir.AxisListType.X, op=ALU.max, negate=True)
@@ -177,8 +178,8 @@ def tile_attend_additivekeys_kernel(tc, query, ba_words, ba_scales, bb_words, bb
 
         inv_sum = sbuf([P, 1], F32, "inv_sum")
         nc.vector.reciprocal(out=inv_sum[:], in_=row_sum[:])
-        codes = sbuf([P, 5 * P], U32, "codes", "picked1_1")
-        plane = sbuf([P, 5 * P], U8, "plane")
+        codes = sbuf([P, 4 * P], U32, "codes", "picked1_1")
+        plane = sbuf([P, 4 * P], U8, "plane")
 
         def quantise(place, count, woven):
             cols = slice(place * P, (place + count) * P)
@@ -188,7 +189,7 @@ def tile_attend_additivekeys_kernel(tc, query, ba_words, ba_scales, bb_words, bb
         weights = keep.tile([P, I], BF16)
         nc.vector.scalar_tensor_tensor(out=weights[:], in0=prob[:], scalar=inv_sum[:],
                                        in1=size_bank[:].rearrange("p m t -> p (m t)"), op0=ALU.mult, op1=ALU.mult)
-        weight_bank = psum.tile([P, 2, Q], F32, name="weight_bank")
+        weight_bank = psum.tile([P, 2, Q], F32, name="weight_bank", tag="weight_bank")
         for u in range(2):
             nc.tensor.transpose(weight_bank[:, u, :], weights[:].bitcast(F32)[:, u::2], ident[:])
 
@@ -220,7 +221,20 @@ def tile_attend_additivekeys_kernel(tc, query, ba_words, ba_scales, bb_words, bb
         finish(1, 2, 4, "scores")
         quantise(3, 1, middle[:, 2].rearrange("p x t -> p (x t)"))
         finish(3, 1, 2, "size_bank")
-        woven0 = sbuf([P, P, PACK], BF16, "woven0")
-        scale_values(0, woven0[:])
-        quantise(4, 1, woven0[:].rearrange("p x t -> p (x t)"))
-        finish(4, 0, 1, "last_bank")
+        half = P // 2
+        halves = range(2)
+        woven0 = [sbuf([P, half, PACK], BF16, "woven0_%d" % h) for h in halves]
+        late_codes = [sbuf([P, half], U32, "late_codes%d" % h) for h in halves]
+        late_plane = [sbuf([P, half], U8, "late_plane%d" % h) for h in halves]
+        late_result = keep.tile([P, P], F32)
+        for h in halves:
+            scale_values(0, woven0[h][:], h * half, (h + 1) * half)
+        for h, tag, copy in ((0, "weight_bank", nc.scalar.copy), (1, "last_bank", nc.vector.tensor_copy)):
+            nc.vector.quantize_mx(out=late_codes[h][:].bitcast(FP8X4), scales=late_plane[h][:],
+                                  in_=woven0[h][:].rearrange("p x t -> p (x t)"))
+            late_bank = psum.tile([P, half], F32, name="late_" + tag, tag=tag)
+            nc.tensor.matmul_mx(out=late_bank[:], lhsT=codes[:, :P].bitcast(FP8X4), lhsT_scale=plane[:, :P],
+                                rhs=late_codes[h][:].bitcast(FP8X4), rhs_scale=late_plane[h][:],
+                                start=True, stop=True)
+            copy(out=late_result[:, h * half:(h + 1) * half], in_=late_bank[:])
+        nc.sync.dma_start(out=out[:, :P], in_=late_result[:])

@@ -23,6 +23,7 @@ E_TILES = E // P
 WORD_WINDOW = U + 177
 BYTE_WINDOW = U + 180
 FLOAT_WINDOW = U + 8
+SCALAR_SHARE = 352
 
 
 def tile_attend_additivekeys_kernel(tc, query, ba_words, ba_scales, bb_words, bb_scales, bc_words, bc_scales,
@@ -143,17 +144,17 @@ def tile_attend_additivekeys_kernel(tc, query, ba_words, ba_scales, bb_words, bb
         gather_words(0)
         load_values(0, 1, "key_words0")
         turn_in_list_order(2, gather_on_scalar(0, 2), True, False)
-        load_values(2, 1, rooms[0, 2])
+        load_values(2, 0, rooms[0, 2], WORD_WINDOW)
         q_bf = sbuf([P, Q, PACK], BF16, "q_bf")
         nc.gpsimd.tensor_copy(out=q_bf[:], in_=q_raw[:].rearrange("p j w -> p w j"))
         gather_words(1)
-        load_values(0, 0, "key_words1")
+        load_values(2, 1, "key_words1")
         q_codes = sbuf([P, Q], U32, "q_codes")
         q_scale = sbuf([P, Q], U8, "q_scale")
         nc.vector.quantize_mx(out=q_codes[:].bitcast(FP8X4), scales=q_scale[:],
                               in_=q_bf[:].rearrange("p w j -> p (w j)"))
         second2 = gather_on_scalar(1, 2)
-        load_values(2, 0, rooms[1, 2], WORD_WINDOW)
+        load_values(0, 0, rooms[1, 2])
         gather_words(2)
         load_values(1, 0, "key_words2")
         woven3 = sbuf([P, P, PACK], BF16, "woven3")
@@ -174,6 +175,10 @@ def tile_attend_additivekeys_kernel(tc, query, ba_words, ba_scales, bb_words, bb
         prob = sbuf([P, I], F32, "prob")
         row_sum = keep.tile([P, 1], F32)
         nc.scalar.activation(out=prob[:], in_=scores[:], func=ACT.Exp, bias=neg_max[:], accum_out=row_sum[:])
+        dealt = sbuf([P, PACK, P], F32, "dealt")
+        nc.vector.tensor_copy(out=dealt[:].bitcast(U32).rearrange("p t m -> p m t"),
+                              in_=tables[2, 0][:].bitcast(U32).indirect(lists[2][:]))
+        turn(0, [dealt[:, t, :] for t in range(PACK)], True, False)
         turn_in_list_order(1, gather_and_add(1, second1), False, True)
 
         inv_sum = sbuf([P, 1], F32, "inv_sum")
@@ -193,15 +198,15 @@ def tile_attend_additivekeys_kernel(tc, query, ba_words, ba_scales, bb_words, bb
         for u in range(2):
             nc.tensor.transpose(weight_bank[:, u, :], weights[:].bitcast(F32)[:, u::2], ident[:])
 
-        turn_in_list_order(0, gather_on_scalar(0, 0), True, False)
-        second0 = gather_on_scalar(1, 0)
-        dealt = sbuf([P, PACK, P], F32, "dealt")
-        nc.vector.tensor_copy(out=dealt[:].bitcast(U32).rearrange("p t m -> p m t"),
-                              in_=tables[2, 0][:].bitcast(U32).indirect(lists[2][:]))
-        turn(0, [dealt[:, t, :] for t in range(PACK)], False, False)
+        turn_in_list_order(0, gather_on_scalar(0, 0), False, False)
+        second0 = sbuf([P, I], F32, "picked1_0")
+        nc.scalar.activation(out=second0[:, :SCALAR_SHARE],
+                             in_=tables[1, 0][:].indirect(lists[1][:, :SCALAR_SHARE // 16]), func=ACT.Copy)
+        nc.vector.tensor_copy(out=second0[:, SCALAR_SHARE:],
+                              in_=tables[1, 0][:].indirect(lists[1][:, SCALAR_SHARE // 16:]))
         turn_in_list_order(0, second0, False, True)
 
-        middle = sbuf([P, 3, P, PACK], BF16, "middle", "prob")
+        middle = sbuf([P, 3, P, PACK], BF16, "middle", rooms[2, 1])
         nc.scalar.copy(out=middle[:, 0].rearrange("p q t -> p (q t)").bitcast(F32).rearrange("p (q u) -> p q u", u=2),
                        in_=weight_bank[:].rearrange("p u q -> p q u"))
 

from contextlib import ExitStack

import concourse.mybir as mybir
from concourse.masks import make_identity

D, I, Q, E, U = 512, 512, 128, 512, 512
FLOPS = 2 * Q * I * D * 3 + 2 * Q * I * E

F32 = mybir.dt.float32
BF16 = mybir.dt.bfloat16
I32 = mybir.dt.int32
U32 = mybir.dt.uint32
U16 = mybir.dt.uint16
U8 = mybir.dt.uint8
FP8X4 = mybir.dt.float8_e4m3fn_x4
ACT = mybir.ActivationFunctionType
ALU = mybir.AluOpType

P = 128
PACK = 4
BLOCKS = 16
E_TILES = E // P
WORD_WINDOW = U + 177
BYTE_WINDOW = U + 180
FLOAT_WINDOW = U + 8
SCALAR_SHARE = 352


def tile_attend_additivekeys_kernel(tc, query, ba_words, ba_scales, bb_words, bb_scales, bc_words, bc_scales,
                                         size, ca, cb, cc, vsc, offs, offs2, offs3, out):
    nc = tc.nc
    lists_in = (offs, offs2, offs3)
    words_in = (ba_words, bb_words, bc_words)
    scales_in = (ba_scales, bb_scales, bc_scales)
    values_in = (ca, cb, cc)
    books = range(3)

    with ExitStack() as ctx:
        keep = ctx.enter_context(tc.tile_pool(name="keep", bufs=1))
        psum = ctx.enter_context(tc.psum_pool(name="psum", bufs=1))

        def sbuf(shape, dtype, name, over=None):
            return keep.tile(shape, dtype, name=name, tag=over or name, align_bytes=64)

        lists = [keep.tile([P, I // 16], U16, name="list%d" % k) for k in books]
        key_words = [sbuf([P, WORD_WINDOW], I32, "key_words%d" % k) for k in books]
        key_bytes = [sbuf([P, BYTE_WINDOW], U8, "key_bytes%d" % k) for k in books]
        first_row = P - BLOCKS
        tables = {}
        rooms = {}

        def load_list(k):
            nc.sync.dma_start(lists[k][:], lists_in[k])

        def load_values(k, g, over=None, width=FLOAT_WINDOW):
            rooms[k, g] = over or "table%d_%d" % (k, g)
            tables[k, g] = sbuf([P, width], F32, "table%d_%d" % (k, g), rooms[k, g])
            nc.sync.dma_start(out=tables[k, g][:, :U], in_=values_in[k][g * P:(g + 1) * P, :])

        def load_words(k):
            nc.sync.dma_start(out=key_words[k][:, :U],
                              in_=words_in[k][0].rearrange("p n t -> p (n t)").bitcast(I32))

        def load_bytes(k):
            nc.sync.dma_start(out=key_bytes[k][first_row:, :U].bitcast(I32), in_=scales_in[k][0].bitcast(I32))

        for k in books:
            load_list(k)
            if k < 2:
                load_bytes(k)
            load_values(k, 3)
        load_bytes(2)
        q_raw = sbuf([P, PACK, Q], F32, "q_raw")
        nc.sync.dma_start(out=q_raw[:], in_=query.rearrange("(p j) w -> p j w", j=PACK))
        load_words(0)
        load_values(0, 2)
        slot_size = sbuf([P, PACK], F32, "slot_size")
        nc.sync.dma_start(out=slot_size[:], in_=size.rearrange("o (p t) -> (o p) t", t=PACK))
        load_words(1)
        load_values(1, 2)
        load_words(2)
        slot_scale = sbuf([P, PACK], F32, "slot_scale")
        nc.sync.dma_start(out=slot_scale[:], in_=vsc.rearrange("(p t) o -> p (t o)", t=PACK))

        for k in books:
            nc.vector.memset(key_bytes[k][:first_row, :U + 4].bitcast(I32), 0)

        warm = keep.tile([P, 1], F32)
        nc.gpsimd.memset(warm[:], 0.0)
        warmed = keep.tile([P, 1], F32)
        nc.scalar.activation(out=warmed[:], in_=warm[:], func=ACT.Exp)
        ident = keep.tile([P, P], F32)
        make_identity(nc, ident[:])

        banks = [psum.tile([P, PACK, P], F32, name="value_bank%d" % g) for g in range(E_TILES)]

        def gather_on_scalar(k, g, over=None):
            picked = sbuf([P, I], F32, "picked%d_%d" % (k, g), over)
            nc.scalar.activation(out=picked[:], in_=tables[k, g][:].indirect(lists[k][:]), func=ACT.Copy)
            return picked

        def turn(g, places, opens, closes):
            for t in range(PACK):
                nc.tensor.matmul(banks[g][:, t, :], lhsT=places[t], rhs=ident[:], is_transpose=True,
                                 start=(opens and t == 0), stop=(closes and t == PACK - 1))

        def turn_in_list_order(g, picked, opens, closes):
            turn(g, [picked[:, t::PACK] for t in range(PACK)], opens, closes)

        def gather_and_add(g, second):
            both = sbuf([P, I], F32, "both%d" % g)
            nc.vector.tensor_tensor(out=both[:], in0=tables[2, g][:].indirect(lists[2][:]), in1=second[:], op=ALU.add)
            return both

        def scale_values(g, woven, lo=0, hi=P):
            nc.vector.tensor_tensor(
                out=woven.rearrange("p (c i) t -> p c t i", i=PACK),
                in0=banks[g][:, :, lo:hi].rearrange("p t (c i) -> p c t i", i=PACK),
                in1=slot_scale[:].rearrange("p (c t i) -> p c t i", c=1, i=1).to_broadcast(
                    [P, (hi - lo) // PACK, PACK, PACK]),
                op=ALU.mult)

        picked_bytes = keep.tile([P, 3 * I], U8)
        for k in books:
            nc.vector.tensor_copy(out=picked_bytes[:, k * I:(k + 1) * I], in_=key_bytes[k][:].indirect(lists[k][:]))
        turn_in_list_order(3, gather_on_scalar(0, 3), True, False)
        planes = sbuf([P, 3 * I], U8, "planes", rooms[0, 3])
        for quad in range(4):
            nc.sync.dma_start(out=planes[32 * quad:32 * quad + 4, :].bitcast(I32),
                              in_=picked_bytes[first_row + 4 * quad:first_row + 4 * quad + 4, :].bitcast(I32))
        load_values(2, 2, "key_bytes2")
        turn_in_list_order(3, gather_on_scalar(1, 3), False, False)
        size_bank = psum.tile([P, P, PACK], F32, name="size_bank", tag="size_bank")
        for t in range(PACK):
            nc.tensor.transpose(size_bank[:, :, t], slot_size[:, t:t + 1].to_broadcast([P, P]), ident[:])
        turn_in_list_order(3, gather_on_scalar(2, 3), False, True)
        load_values(1, 1, rooms[2, 3])

        picked_words = [sbuf([P, I], U32, "picked_words%d" % k) for k in books]

        def gather_words(k):
            nc.vector.tensor_copy(out=picked_words[k][:], in_=key_words[k][:].bitcast(U32).indirect(lists[k][:]))

        gather_words(0)
        load_values(0, 1, "key_words0")
        turn_in_list_order(2, gather_on_scalar(0, 2), True, False)
        load_values(2, 0, rooms[0, 2], WORD_WINDOW)
        q_bf = sbuf([P, Q, PACK], BF16, "q_bf")
        nc.gpsimd.tensor_copy(out=q_bf[:], in_=q_raw[:].rearrange("p j w -> p w j"))
        gather_words(1)
        load_values(2, 1, "key_words1")
        q_codes = sbuf([P, Q], U32, "q_codes")
        q_scale = sbuf([P, Q], U8, "q_scale")
        nc.vector.quantize_mx(out=q_codes[:].bitcast(FP8X4), scales=q_scale[:],
                              in_=q_bf[:].rearrange("p w j -> p (w j)"))
        second2 = gather_on_scalar(1, 2)
        load_values(0, 0, rooms[1, 2])
        gather_words(2)
        load_values(1, 0, "key_words2")
        woven3 = sbuf([P, P, PACK], BF16, "woven3")
        scale_values(3, woven3[:])

        scores = psum.tile([P, I], F32, name="scores", tag="scores")
        for k in books:
            nc.tensor.matmul_mx(out=scores[:], lhsT=q_codes[:].bitcast(FP8X4), lhsT_scale=q_scale[:],
                                rhs=picked_words[k][:].bitcast(FP8X4), rhs_scale=planes[:, k * I:(k + 1) * I],
                                start=(k == 0), stop=(k == 2))

        second1 = gather_on_scalar(1, 1)
        both2 = gather_and_add(2, second2)
        neg_max = sbuf([P, 1], F32, "neg_max")
        nc.vector.tensor_reduce(out=neg_max[:], in_=scores[:], axis=mybir.AxisListType.X, op=ALU.max, negate=True)
        turn_in_list_order(2, both2, False, True)
        turn_in_list_order(1, gather_on_scalar(0, 1), True, False)
        prob = sbuf([P, I], F32, "prob")
        row_sum = keep.tile([P, 1], F32)
        nc.scalar.activation(out=prob[:], in_=scores[:], func=ACT.Exp, bias=neg_max[:], accum_out=row_sum[:])
        dealt = sbuf([P, PACK, P], F32, "dealt")
        nc.vector.tensor_copy(out=dealt[:].bitcast(U32).rearrange("p t m -> p m t"),
                              in_=tables[2, 0][:].bitcast(U32).indirect(lists[2][:]))
        turn(0, [dealt[:, t, :] for t in range(PACK)], True, False)
        turn_in_list_order(1, gather_and_add(1, second1), False, True)

        inv_sum = sbuf([P, 1], F32, "inv_sum")
        nc.vector.reciprocal(out=inv_sum[:], in_=row_sum[:])
        codes = sbuf([P, 4 * P], U32, "codes", "picked1_1")
        plane = sbuf([P, 4 * P], U8, "plane")

        def quantise(place, count, woven):
            cols = slice(place * P, (place + count) * P)
            nc.vector.quantize_mx(out=codes[:, cols].bitcast(FP8X4), scales=plane[:, cols], in_=woven)

        quantise(2, 1, woven3[:].rearrange("p x t -> p (x t)"))
        weights = keep.tile([P, I], BF16)
        nc.vector.scalar_tensor_tensor(out=weights[:], in0=prob[:], scalar=inv_sum[:],
                                       in1=size_bank[:].rearrange("p m t -> p (m t)"), op0=ALU.mult, op1=ALU.mult)
        weight_bank = psum.tile([P, 2, Q], F32, name="weight_bank", tag="weight_bank")
        for u in range(2):
            nc.tensor.transpose(weight_bank[:, u, :], weights[:].bitcast(F32)[:, u::2], ident[:])

        turn_in_list_order(0, gather_on_scalar(0, 0), False, False)
        second0 = sbuf([P, I], F32, "picked1_0")
        nc.scalar.activation(out=second0[:, :SCALAR_SHARE],
                             in_=tables[1, 0][:].indirect(lists[1][:, :SCALAR_SHARE // 16]), func=ACT.Copy)
        nc.vector.tensor_copy(out=second0[:, SCALAR_SHARE:],
                              in_=tables[1, 0][:].indirect(lists[1][:, SCALAR_SHARE // 16:]))
        turn_in_list_order(0, second0, False, True)

        middle = sbuf([P, 3, P, PACK], BF16, "middle", rooms[2, 1])
        nc.scalar.copy(out=middle[:, 0].rearrange("p q t -> p (q t)").bitcast(F32).rearrange("p (q u) -> p q u", u=2),
                       in_=weight_bank[:].rearrange("p u q -> p q u"))

        def finish(place, lo, hi, tag):
            cols = slice(place * P, (place + hi - lo) * P)
            result_bank = psum.tile([P, (hi - lo) * P], F32, name="result_" + tag, tag=tag)
            nc.tensor.matmul_mx(out=result_bank[:], lhsT=codes[:, :P].bitcast(FP8X4), lhsT_scale=plane[:, :P],
                                rhs=codes[:, cols].bitcast(FP8X4), rhs_scale=plane[:, cols],
                                start=True, stop=True)
            result = keep.tile([P, (hi - lo) * P], F32, name="result%d" % lo)
            nc.scalar.copy(out=result[:], in_=result_bank[:])
            nc.sync.dma_start(out=out[:, lo * P:hi * P], in_=result[:])

        scale_values(2, middle[:, 1])
        scale_values(1, middle[:, 2])
        quantise(0, 2, middle[:, :2].rearrange("p g x t -> p (g x t)"))
        finish(1, 2, 4, "scores")
        quantise(3, 1, middle[:, 2].rearrange("p x t -> p (x t)"))
        finish(3, 1, 2, "size_bank")
        half = P // 2
        halves = range(2)
        woven0 = [sbuf([P, half, PACK], BF16, "woven0_%d" % h) for h in halves]
        late_codes = [sbuf([P, half], U32, "late_codes%d" % h) for h in halves]
        late_plane = [sbuf([P, half], U8, "late_plane%d" % h) for h in halves]
        late_result = keep.tile([P, P], F32)
        for h in halves:
            scale_values(0, woven0[h][:], h * half, (h + 1) * half)
        for h, tag, copy in ((0, "weight_bank", nc.scalar.copy), (1, "last_bank", nc.vector.tensor_copy)):
            nc.vector.quantize_mx(out=late_codes[h][:].bitcast(FP8X4), scales=late_plane[h][:],
                                  in_=woven0[h][:].rearrange("p x t -> p (x t)"))
            late_bank = psum.tile([P, half], F32, name="late_" + tag, tag=tag)
            nc.tensor.matmul_mx(out=late_bank[:], lhsT=codes[:, :P].bitcast(FP8X4), lhsT_scale=plane[:, :P],
                                rhs=late_codes[h][:].bitcast(FP8X4), rhs_scale=late_plane[h][:],
                                start=True, stop=True)
            copy(out=late_result[:, h * half:(h + 1) * half], in_=late_bank[:])
        nc.sync.dma_start(out=out[:, :P], in_=late_result[:])
